import numpy as np
import ml_dtypes


def mxq(x, axis, fmt="e4m3"):
    dtype, down = {"e4m3": (ml_dtypes.float8_e4m3fn, 7), "e5m2": (ml_dtypes.float8_e5m2, 14)}[fmt]
    v = np.moveaxis(np.asarray(x, np.float32).astype(ml_dtypes.bfloat16).astype(np.float64), axis, -1)
    blocks = v.reshape(v.shape[:-1] + (-1, 32))
    amax = np.abs(blocks).max(-1, keepdims=True)
    byte = np.maximum(np.where(amax > 0, np.frexp(amax)[1] - 1 + 127, 0) - down, 1)
    scale = np.exp2(byte - 127.0)
    codes = (blocks / scale).astype(np.float32).astype(dtype).astype(np.float64)
    return np.moveaxis((codes * scale).reshape(v.shape), -1, axis)


WIDE = False


def mx_kscale(k):
    if not WIDE:
        return np.ones(k)
    levels = np.array([10, -10, 5, -5, 0])
    if k % 512:
        return np.exp2(np.random.permutation(np.resize(levels, k // 32))).repeat(32)
    a = np.empty((k // 512, 16))
    for p in range(k // 512):
        a[p, :8] = np.random.permutation(np.resize(levels, 8))
        for g in range(8):
            far = levels[np.abs(levels - a[p, g]) >= 10]
            a[p, g + 8] = far[np.random.randint(len(far))]
    return np.exp2(a.ravel()).repeat(32)


def f64(x):
    return np.asarray(x).astype(np.float64)


def striped8(idx):
    return np.concatenate([v.reshape(-1, 16).T for v in idx]).astype(np.uint16)


def unstriped8(offs):
    return np.stack([offs[16 * g:16 * g + 16].T.reshape(-1) for g in range(8)]).astype(np.int64)


E2M1 = np.array([0.0, 0.5, 1.0, 1.5, 2.0, 3.0, 4.0, 6.0, -0.0, -0.5, -1.0, -1.5, -2.0, -3.0, -4.0, -6.0])


def pack_weight(w, fmt):
    k, n = w.shape
    w = f64(np.asarray(w, np.float32).astype(ml_dtypes.bfloat16)).reshape(k // 32, 32, n)
    amax = np.abs(w).max(1)
    if fmt == "e4m3":
        byte = np.frexp(amax)[1] - 1 + 127 - 7
    else:
        mant, ex = np.frexp(amax / 6.0)
        byte = np.where(mant > 0.5, ex, ex - 1) + 127
    byte = np.clip(np.where(amax > 0, byte, 1), 1, 254)
    scaled = (w * np.exp2(127.0 - byte)[:, None, :]).reshape(k, n).astype(np.float32)
    by_word = np.ascontiguousarray(scaled.reshape(k // 512, 128, 4, n).transpose(0, 1, 3, 2))
    if fmt == "e4m3":
        words = by_word.astype(ml_dtypes.float8_e4m3fn).view(np.uint8)
    else:
        c = by_word.astype(ml_dtypes.float4_e2m1fn).view(np.uint8) & 0xF
        words = (c[..., 0::2] | (c[..., 1::2] << 4)).reshape(k // 512, 128, 2 * n)
    return np.ascontiguousarray(words), np.ascontiguousarray(byte.astype(np.uint8).reshape(k // 512, 16, n))


def unpack_weight(words, scales, fmt):
    g, _, n = scales.shape
    words = np.ascontiguousarray(words).reshape(g, 128, n, -1)
    if fmt == "e4m3":
        vals = words.view(ml_dtypes.float8_e4m3fn).astype(np.float64)
    else:
        nib = np.empty((g, 128, n, 4), np.uint8)
        nib[..., 0::2] = words & 0xF
        nib[..., 1::2] = words >> 4
        vals = E2M1[nib]
    vals = vals * np.repeat(np.exp2(scales.astype(np.float64) - 127.0), 8, axis=1)[..., None]
    return vals.transpose(0, 1, 3, 2).reshape(g * 512, n)


def gelu(v):
    return 0.5 * v * (1.0 + np.tanh(np.sqrt(2.0 / np.pi) * (v + 0.044715 * v**3)))


K, L, M, T, S = 1536, 1024, 512, 1024, 512


def setup_inputs():
    n = np.random.standard_normal
    s1 = mx_kscale(K)[:, None]
    s2 = mx_kscale(L)[:, None]
    p_w4 = pack_weight(n((K, M)) / np.sqrt(K) / s1, "e2m1")
    return {
        "xT": (n((K, T)) * s1).astype(np.float32),
        "w4_words": p_w4[0],
        "w4_scales": p_w4[1],
        "c": (n((L, S)) * s2).astype(np.float32),
        "u": (n((L, M)) / np.sqrt(L) / s2).astype(np.float32),
        "wgt": np.repeat(np.random.uniform(0.5, 2.0, (8, S)), 16, axis=0).astype(np.float32),
        "b": (0.3 * n(512)).astype(np.float32),
        "offs": striped8(np.stack([np.random.permutation(T)[:S] for _ in range(8)])),
    }


def reference(xT, w4_words, w4_scales, c, u, wgt, b, offs):
    idx = unstriped8(offs)
    group = np.arange(K) % 512 // 64
    xg = f64(wgt)[np.arange(K) // 4 % 128] * f64(xT)[np.arange(K)[:, None], idx[group]]
    xT_ = mxq(xg, 0, "e4m3")
    w4_ = unpack_weight(w4_words, w4_scales, "e2m1")
    c_ = mxq(f64(c), 0, "e4m3")
    u_ = mxq(f64(u), 0, "e4m3")
    y = w4_.T @ xT_ + u_.T @ c_
    return gelu(y + f64(b)[:, None])

@@ -1,0 +1,209 @@
+from contextlib import ExitStack
+
+import concourse.mybir as mybir
+from concourse.masks import make_identity
+
+K, L, M, T, S = 1536, 1024, 512, 1024, 512
+FLOPS = 2 * M * S * (K + L)
+
+F32 = mybir.dt.float32
+BF16 = mybir.dt.bfloat16
+I32 = mybir.dt.int32
+U32 = mybir.dt.uint32
+U16 = mybir.dt.uint16
+U8 = mybir.dt.uint8
+FP8X4 = mybir.dt.float8_e4m3fn_x4
+FP4X4 = mybir.dt.float4_e2m1fn_x4
+MULT = mybir.AluOpType.mult
+GELU = mybir.ActivationFunctionType.Gelu_apprx_tanh
+
+P = 128
+KP = 512
+NX, NC = K // KP, L // KP
+NM = M // P
+H = S // 2
+LATE = M - P
+
+
+def tile_list_hmix_gelu_kernel(tc, xT, w4_words, w4_scales, c, u, wgt, b, offs, out):
+    nc = tc.nc
+    with ExitStack() as ctx:
+        keep = ctx.enter_context(tc.tile_pool(name="keep", bufs=1))
+        psum = ctx.enter_context(tc.psum_pool(name="psum", bufs=1))
+
+        def held(shape, dtype, name):
+            return keep.tile(shape, dtype, name=name, tag=name, align_bytes=64)
+
+        offsets = keep.tile([P, S // 16], U16, name="offsets")
+        weight = held([P, S], F32, "weight")
+        planes = [[held([P, T], F32, "plane%d_%d" % (a, i)) for i in range(4)] for a in range(NX)]
+        picked = [held([P, 4, S], F32, "picked%d" % a) for a in range(NX)]
+        c_raw = [held([P, 4, S], F32, "c_raw%d" % a) for a in range(NC)]
+        u_raw = [held([P, 4, M], F32, "u_raw%d" % a) for a in range(NC)]
+        x_mix = [held([P, S, 4], BF16, "x_mix%d" % a) for a in range(NX)]
+        c_mix = [held([P, S, 4], BF16, "c_mix%d" % a) for a in range(NC)]
+        u_mix = [held([P, M, 4], BF16, "u_mix%d" % a) for a in range(NC)]
+        x_codes = [None] * NX
+        c_codes = [None] * NC
+        u_codes = [held([P, M], U32, "u_codes%d" % a) for a in range(NC)]
+        x_scale = [held([P, S], U8, "x_scale%d" % a) for a in range(NX)]
+        c_scale = [held([P, S], U8, "c_scale%d" % a) for a in range(NC)]
+        u_scale = [held([P, M], U8, "u_scale%d" % a) for a in range(NC)]
+        w_words = held([P, NX, 2 * M], U8, "w_words")
+        w_scale = held([P, NX, M], U8, "w_scale")
+        b_rows = held([P, P], F32, "b_rows")
+        b_cols = held([P, NM], F32, "b_cols")
+        ident = held([P, P], F32, "ident")
+        warm = held([P, 1], F32, "warm")
+        result = [held([P, S], F32, "result%d" % m) for m in range(NM)]
+        sums = [psum.tile([P, S], F32, name="sums%d" % m, tag="sums%d" % m) for m in range(NM)]
+        b_turned = psum.tile([P, P], F32, name="b_turned")
+
+        def instead(tag, shape, dtype, name):
+            return keep.tile(shape, dtype, name=name, tag=tag, align_bytes=64)
+
+        def load_plane(a, i):
+            rows = xT[KP * a : KP * (a + 1), :].rearrange("(p i) t -> p i t", i=4)
+            nc.sync.dma_start(planes[a][i][:], rows[:, i, :])
+
+        def load_w_scale(q):
+            nc.sync.dma_start(
+                w_scale[32 * q : 32 * q + 4, :, :].bitcast(I32),
+                w4_scales[:, 4 * q : 4 * q + 4, :].rearrange("a r n -> r a n").bitcast(I32),
+            )
+
+        def load_raw(tiles, src, a, lo, hi):
+            rows = src[KP * a : KP * (a + 1), :].rearrange("(p i) w -> p i w", i=4)
+            nc.sync.dma_start(tiles[a][:, :, lo:hi], rows[:, :, lo:hi])
+
+        def gather(a, i):
+            for h in range(2):
+                cols = slice(h * H, (h + 1) * H)
+                nc.vector.tensor_tensor(
+                    picked[a][:, i, cols],
+                    planes[a][i][:].indirect(offsets[:, h * H // 16 : (h + 1) * H // 16]),
+                    weight[:, cols],
+                    MULT,
+                )
+
+        def mix(on_scalar, mixed, raw, lo, hi):
+            src = raw[:, :, lo:hi].rearrange("p i (g w) -> p g i w", w=4)
+            dst = mixed[:, lo:hi, :].rearrange("p (g w) i -> p g i w", w=4)
+            if on_scalar:
+                nc.scalar.copy(dst, src)
+            else:
+                nc.vector.tensor_copy(dst, src)
+
+        def quantise(codes, scale, mixed, lo, hi):
+            nc.vector.quantize_mx(
+                out=codes[:, lo:hi].bitcast(FP8X4),
+                scales=scale[:, lo:hi],
+                in_=mixed[:, lo:hi, :].rearrange("p w i -> p (w i)"),
+            )
+
+        def times_w4(a, start):
+            for m in range(NM):
+                nc.tensor.matmul_mx(
+                    out=sums[m][:],
+                    lhsT=w_words[:, a, 2 * P * m : 2 * P * (m + 1)].bitcast(FP4X4),
+                    lhsT_scale=w_scale[:, a, P * m : P * (m + 1)],
+                    rhs=x_codes[a][:].bitcast(FP8X4),
+                    rhs_scale=x_scale[a][:],
+                    start=start,
+                    stop=False,
+                )
+
+        def times_u(a, m, stop):
+            cols = slice(P * m, P * (m + 1))
+            nc.tensor.matmul_mx(
+                out=sums[m][:],
+                lhsT=u_codes[a][:, cols].bitcast(FP8X4),
+                lhsT_scale=u_scale[a][:, cols],
+                rhs=c_codes[a][:].bitcast(FP8X4),
+                rhs_scale=c_scale[a][:],
+                start=False,
+                stop=stop,
+            )
+
+        def finish(m, pieces):
+            width = S // pieces
+            for j in range(pieces):
+                cols = slice(width * j, width * (j + 1))
+                nc.scalar.activation(result[m][:, cols], sums[m][:, cols], GELU, bias=b_cols[:, m : m + 1])
+                nc.sync.dma_start(out[P * m : P * (m + 1), cols], result[m][:, cols])
+
+        nc.gpsimd.memset(w_scale[:].rearrange("p a n -> p (a n)").bitcast(I32), 0)
+        nc.gpsimd.memset(b_rows[:], 0.0)
+        nc.gpsimd.memset(warm[:], 0.0)
+        make_identity(nc, ident[:])
+        nc.scalar.activation(warm[:], warm[:], GELU)
+
+        nc.sync.dma_start(offsets[:], offs)
+        nc.sync.dma_start(weight[:, 0:H], wgt[:, 0:H])
+        load_plane(0, 0)
+        nc.sync.dma_start(weight[:, H:S], wgt[:, H:S])
+        for i in range(1, 4):
+            load_plane(0, i)
+        for i in range(3):
+            load_plane(1, i)
+            load_w_scale(i)
+        load_raw(c_raw, c, 0, 0, S)
+        load_w_scale(3)
+        load_plane(1, 3)
+        nc.sync.dma_start(b_rows[0:NM, :], b.rearrange("(m p) -> m p", p=P))
+        for i in range(3):
+            load_plane(2, i)
+        load_raw(c_raw, c, 1, 0, S)
+        load_plane(2, 3)
+        nc.sync.dma_start(w_words[:], w4_words.rearrange("a p n -> p a n"))
+        load_raw(u_raw, u, 0, 0, M)
+        load_raw(u_raw, u, 1, 0, H)
+        load_raw(u_raw, u, 1, H, M)
+
+        for i in range(4):
+            gather(0, i)
+        mix(True, x_mix[0], picked[0], 0, S)
+        for i in range(3):
+            gather(1, i)
+        mix(True, c_mix[0], c_raw[0], 0, S)
+        x_codes[0] = instead("plane1_2", [P, S], U32, "x_codes0")
+        quantise(x_codes[0], x_scale[0], x_mix[0], 0, S)
+        gather(1, 3)
+        mix(True, x_mix[1], picked[1], 0, S)
+        for i in range(3):
+            gather(2, i)
+        x_codes[1] = instead("plane2_2", [P, S], U32, "x_codes1")
+        quantise(x_codes[1], x_scale[1], x_mix[1], 0, S)
+        mix(True, c_mix[1], c_raw[1], 0, S)
+        nc.tensor.transpose(b_turned[:], b_rows[:], ident[:])
+        nc.scalar.copy(b_cols[:], b_turned[:, 0:NM])
+        gather(2, 3)
+        mix(False, x_mix[2], picked[2], 0, H)
+        mix(True, x_mix[2], picked[2], H, S)
+        c_codes[0] = instead("plane2_3", [P, S], U32, "c_codes0")
+        c_codes[1] = held([P, S], U32, "c_codes1")
+        quantise(c_codes[0], c_scale[0], c_mix[0], 0, S)
+        quantise(c_codes[1], c_scale[1], c_mix[1], 0, S)
+        times_w4(0, True)
+        times_w4(1, False)
+        x_codes[2] = held([P, S], U32, "x_codes2")
+        quantise(x_codes[2], x_scale[2], x_mix[2], 0, S)
+        times_w4(2, False)
+        mix(True, u_mix[0], u_raw[0], 0, H)
+        mix(True, u_mix[0], u_raw[0], H, M)
+        mix(False, u_mix[1], u_raw[1], 0, H)
+        quantise(u_codes[0], u_scale[0], u_mix[0], 0, H)
+        quantise(u_codes[1], u_scale[1], u_mix[1], 0, H)
+        mix(True, u_mix[1], u_raw[1], H, LATE)
+        mix(False, u_mix[1], u_raw[1], LATE, M)
+        for m in (0, 1):
+            times_u(0, m, False)
+            times_u(1, m, True)
+            finish(m, 1)
+        quantise(u_codes[0], u_scale[0], u_mix[0], H, M)
+        quantise(u_codes[1], u_scale[1], u_mix[1], H, LATE)
+        quantise(u_codes[1], u_scale[1], u_mix[1], LATE, M)
+        for m in (2, 3):
+            times_u(0, m, False)
+            times_u(1, m, True)
+            finish(m, m - 1)

@@ -22,7 +22,7 @@ KP = 512
 NX, NC = K // KP, L // KP
 NM = M // P
 H = S // 2
-LATE = M - P
+U_PIECES = ((0, 2 * P), (2 * P, 3 * P), (3 * P, 4 * P))
 
 
 def tile_list_hmix_gelu_kernel(tc, xT, w4_words, w4_scales, c, u, wgt, b, offs, out):
@@ -31,20 +31,20 @@ def tile_list_hmix_gelu_kernel(tc, xT, w4_words, w4_scales, c, u, wgt, b, offs, 
         keep = ctx.enter_context(tc.tile_pool(name="keep", bufs=1))
         psum = ctx.enter_context(tc.psum_pool(name="psum", bufs=1))
 
-        def held(shape, dtype, name):
-            return keep.tile(shape, dtype, name=name, tag=name, align_bytes=64)
+        def held(shape, dtype, name, tag=None):
+            return keep.tile(shape, dtype, name=name, tag=tag or name, align_bytes=64)
 
         offsets = keep.tile([P, S // 16], U16, name="offsets")
-        weight = held([P, S], F32, "weight")
+        weight_all = held([P, S], F32, "weight_all")
+        weight = [weight_all[:, 0:H], weight_all[:, H:S]]
         planes = [[held([P, T], F32, "plane%d_%d" % (a, i)) for i in range(4)] for a in range(NX)]
         picked = [held([P, 4, S], F32, "picked%d" % a) for a in range(NX)]
-        c_raw = [held([P, 4, S], F32, "c_raw%d" % a) for a in range(NC)]
-        u_raw = [held([P, 4, M], F32, "u_raw%d" % a) for a in range(NC)]
+        c_first = [held([P, 4, H], F32, "c_first%d" % h) for h in range(2)]
+        c_second = held([P, 4, S], F32, "c_second")
+        u_raw = [[held([P, 4, hi - lo], F32, "u_raw%d_%d" % (a, lo)) for a in range(NC)] for lo, hi in U_PIECES]
         x_mix = [held([P, S, 4], BF16, "x_mix%d" % a) for a in range(NX)]
         c_mix = [held([P, S, 4], BF16, "c_mix%d" % a) for a in range(NC)]
         u_mix = [held([P, M, 4], BF16, "u_mix%d" % a) for a in range(NC)]
-        x_codes = [None] * NX
-        c_codes = [None] * NC
         u_codes = [held([P, M], U32, "u_codes%d" % a) for a in range(NC)]
         x_scale = [held([P, S], U8, "x_scale%d" % a) for a in range(NX)]
         c_scale = [held([P, S], U8, "c_scale%d" % a) for a in range(NC)]
@@ -59,71 +59,25 @@ def tile_list_hmix_gelu_kernel(tc, xT, w4_words, w4_scales, c, u, wgt, b, offs, 
         sums = [psum.tile([P, S], F32, name="sums%d" % m, tag="sums%d" % m) for m in range(NM)]
         b_turned = psum.tile([P, P], F32, name="b_turned")
 
-        def instead(tag, shape, dtype, name):
-            return keep.tile(shape, dtype, name=name, tag=tag, align_bytes=64)
-
-        def load_plane(a, i):
-            rows = xT[KP * a : KP * (a + 1), :].rearrange("(p i) t -> p i t", i=4)
-            nc.sync.dma_start(planes[a][i][:], rows[:, i, :])
-
-        def load_w_scale(q):
-            nc.sync.dma_start(
-                w_scale[32 * q : 32 * q + 4, :, :].bitcast(I32),
-                w4_scales[:, 4 * q : 4 * q + 4, :].rearrange("a r n -> r a n").bitcast(I32),
-            )
-
-        def load_raw(tiles, src, a, lo, hi):
+        def load_rows(tile, src, a, lo, hi):
             rows = src[KP * a : KP * (a + 1), :].rearrange("(p i) w -> p i w", i=4)
-            nc.sync.dma_start(tiles[a][:, :, lo:hi], rows[:, :, lo:hi])
+            nc.sync.dma_start(tile[:], rows[:, :, lo:hi])
 
-        def gather(a, i):
-            for h in range(2):
-                cols = slice(h * H, (h + 1) * H)
-                nc.vector.tensor_tensor(
-                    picked[a][:, i, cols],
-                    planes[a][i][:].indirect(offsets[:, h * H // 16 : (h + 1) * H // 16]),
-                    weight[:, cols],
-                    MULT,
-                )
-
-        def mix(on_scalar, mixed, raw, lo, hi):
-            src = raw[:, :, lo:hi].rearrange("p i (g w) -> p g i w", w=4)
-            dst = mixed[:, lo:hi, :].rearrange("p (g w) i -> p g i w", w=4)
+        def mix(on_scalar, dst, src):
+            src = src.rearrange("p i (g w) -> p g i w", w=4)
+            dst = dst.rearrange("p (g w) i -> p g i w", w=4)
             if on_scalar:
                 nc.scalar.copy(dst, src)
             else:
                 nc.vector.tensor_copy(dst, src)
 
-        def quantise(codes, scale, mixed, lo, hi):
-            nc.vector.quantize_mx(
-                out=codes[:, lo:hi].bitcast(FP8X4),
-                scales=scale[:, lo:hi],
-                in_=mixed[:, lo:hi, :].rearrange("p w i -> p (w i)"),
-            )
+        def mix_shared(dst, src, width):
+            half = width // 2
+            mix(False, dst[:, 0:half, :], src[:, :, 0:half])
+            mix(True, dst[:, half:width, :], src[:, :, half:width])
 
-        def times_w4(a, start):
-            for m in range(NM):
-                nc.tensor.matmul_mx(
-                    out=sums[m][:],
-                    lhsT=w_words[:, a, 2 * P * m : 2 * P * (m + 1)].bitcast(FP4X4),
-                    lhsT_scale=w_scale[:, a, P * m : P * (m + 1)],
-                    rhs=x_codes[a][:].bitcast(FP8X4),
-                    rhs_scale=x_scale[a][:],
-                    start=start,
-                    stop=False,
-                )
-
-        def times_u(a, m, stop):
-            cols = slice(P * m, P * (m + 1))
-            nc.tensor.matmul_mx(
-                out=sums[m][:],
-                lhsT=u_codes[a][:, cols].bitcast(FP8X4),
-                lhsT_scale=u_scale[a][:, cols],
-                rhs=c_codes[a][:].bitcast(FP8X4),
-                rhs_scale=c_scale[a][:],
-                start=False,
-                stop=stop,
-            )
+        def quantise(codes, scale, mixed):
+            nc.vector.quantize_mx(out=codes.bitcast(FP8X4), scales=scale, in_=mixed.rearrange("p w i -> p (w i)"))
 
         def finish(m, pieces):
             width = S // pieces
@@ -139,71 +93,90 @@ def tile_list_hmix_gelu_kernel(tc, xT, w4_words, w4_scales, c, u, wgt, b, offs, 
         nc.scalar.activation(warm[:], warm[:], GELU)
 
         nc.sync.dma_start(offsets[:], offs)
-        nc.sync.dma_start(weight[:, 0:H], wgt[:, 0:H])
-        load_plane(0, 0)
-        nc.sync.dma_start(weight[:, H:S], wgt[:, H:S])
-        for i in range(1, 4):
-            load_plane(0, i)
-        for i in range(3):
-            load_plane(1, i)
-            load_w_scale(i)
-        load_raw(c_raw, c, 0, 0, S)
-        load_w_scale(3)
-        load_plane(1, 3)
-        nc.sync.dma_start(b_rows[0:NM, :], b.rearrange("(m p) -> m p", p=P))
-        for i in range(3):
-            load_plane(2, i)
-        load_raw(c_raw, c, 1, 0, S)
-        load_plane(2, 3)
-        nc.sync.dma_start(w_words[:], w4_words.rearrange("a p n -> p a n"))
-        load_raw(u_raw, u, 0, 0, M)
-        load_raw(u_raw, u, 1, 0, H)
-        load_raw(u_raw, u, 1, H, M)
+        nc.sync.dma_start(weight[0], wgt[:, 0:H])
+        for a in range(NX):
+            rows = xT[KP * a : KP * (a + 1), :].rearrange("(p i) t -> p i t", i=4)
+            for i in range(4):
+                nc.sync.dma_start(planes[a][i][:], rows[:, i, :])
+                if a == 0 and i == 0:
+                    nc.sync.dma_start(weight[1], wgt[:, H:S])
+                if a > 0 and i == 1:
+                    load_rows(c_first[a - 1], c, 0, H * (a - 1), H * a)
+                if a == 1:
+                    nc.sync.dma_start(
+                        w_scale[32 * i : 32 * i + 4, :, :].bitcast(I32),
+                        w4_scales[:, 4 * i : 4 * i + 4, :].rearrange("a r n -> r a n").bitcast(I32),
+                    )
+                if a == NX - 1 and i == 2:
+                    nc.sync.dma_start(b_rows[0:NM, :], b.rearrange("(m p) -> m p", p=P))
+                    nc.sync.dma_start(w_words[:], w4_words.rearrange("a p n -> p a n"))
+        load_rows(c_second, c, 1, 0, S)
+        for piece, (lo, hi) in enumerate(U_PIECES):
+            for a in range(NC):
+                load_rows(u_raw[piece][a], u, a, lo, hi)
 
-        for i in range(4):
-            gather(0, i)
-        mix(True, x_mix[0], picked[0], 0, S)
-        for i in range(3):
-            gather(1, i)
-        mix(True, c_mix[0], c_raw[0], 0, S)
-        x_codes[0] = instead("plane1_2", [P, S], U32, "x_codes0")
-        quantise(x_codes[0], x_scale[0], x_mix[0], 0, S)
-        gather(1, 3)
-        mix(True, x_mix[1], picked[1], 0, S)
-        for i in range(3):
-            gather(2, i)
-        x_codes[1] = instead("plane2_2", [P, S], U32, "x_codes1")
-        quantise(x_codes[1], x_scale[1], x_mix[1], 0, S)
-        mix(True, c_mix[1], c_raw[1], 0, S)
+        x_codes, c_codes = [], []
+        for a in range(NX):
+            for i in range(4):
+                if (a, i) in ((0, 0), (NX - 1, 3)):
+                    for h in range(2):
+                        listed = offsets[:, h * H // 16 : (h + 1) * H // 16]
+                        cols = slice(h * H, (h + 1) * H)
+                        nc.vector.tensor_tensor(picked[a][:, i, cols], planes[a][i][:].indirect(listed), weight[h], MULT)
+                else:
+                    nc.vector.tensor_tensor(
+                        picked[a][:, i, :], planes[a][i][:].indirect(offsets[:]), weight_all[:], MULT
+                    )
+                if a > 0 and i == 1:
+                    x_codes.append(held([P, S], U32, "x_codes%d" % (a - 1), "plane%d_1" % a))
+                    quantise(x_codes[a - 1][:], x_scale[a - 1][:], x_mix[a - 1][:])
+                    mix(True, c_mix[0][:, H * (a - 1) : H * a, :], c_first[a - 1][:])
+                if a == NX - 1 and i == 2:
+                    c_codes.append(held([P, S], U32, "c_codes0", "plane%d_2" % a))
+                    quantise(c_codes[0][:], c_scale[0][:], c_mix[0][:])
+            if a < NX - 1:
+                mix(True, x_mix[a][:], picked[a][:])
+        mix(True, x_mix[NX - 1][:, 0:H, :], picked[NX - 1][:, :, 0:H])
+        mix(False, x_mix[NX - 1][:, H:S, :], picked[NX - 1][:, :, H:S])
+        x_codes.append(held([P, S], U32, "x_codes2"))
+        quantise(x_codes[NX - 1][:], x_scale[NX - 1][:], x_mix[NX - 1][:])
+
         nc.tensor.transpose(b_turned[:], b_rows[:], ident[:])
         nc.scalar.copy(b_cols[:], b_turned[:, 0:NM])
-        gather(2, 3)
-        mix(False, x_mix[2], picked[2], 0, H)
-        mix(True, x_mix[2], picked[2], H, S)
-        c_codes[0] = instead("plane2_3", [P, S], U32, "c_codes0")
-        c_codes[1] = held([P, S], U32, "c_codes1")
-        quantise(c_codes[0], c_scale[0], c_mix[0], 0, S)
-        quantise(c_codes[1], c_scale[1], c_mix[1], 0, S)
-        times_w4(0, True)
-        times_w4(1, False)
-        x_codes[2] = held([P, S], U32, "x_codes2")
-        quantise(x_codes[2], x_scale[2], x_mix[2], 0, S)
-        times_w4(2, False)
-        mix(True, u_mix[0], u_raw[0], 0, H)
-        mix(True, u_mix[0], u_raw[0], H, M)
-        mix(False, u_mix[1], u_raw[1], 0, H)
-        quantise(u_codes[0], u_scale[0], u_mix[0], 0, H)
-        quantise(u_codes[1], u_scale[1], u_mix[1], 0, H)
-        mix(True, u_mix[1], u_raw[1], H, LATE)
-        mix(False, u_mix[1], u_raw[1], LATE, M)
-        for m in (0, 1):
-            times_u(0, m, False)
-            times_u(1, m, True)
-            finish(m, 1)
-        quantise(u_codes[0], u_scale[0], u_mix[0], H, M)
-        quantise(u_codes[1], u_scale[1], u_mix[1], H, LATE)
-        quantise(u_codes[1], u_scale[1], u_mix[1], LATE, M)
-        for m in (2, 3):
-            times_u(0, m, False)
-            times_u(1, m, True)
-            finish(m, m - 1)
+
+        for a in range(NX):
+            for m in range(NM):
+                nc.tensor.matmul_mx(
+                    out=sums[m][:],
+                    lhsT=w_words[:, a, 2 * P * m : 2 * P * (m + 1)].bitcast(FP4X4),
+                    lhsT_scale=w_scale[:, a, P * m : P * (m + 1)],
+                    rhs=x_codes[a][:].bitcast(FP8X4),
+                    rhs_scale=x_scale[a][:],
+                    start=a == 0,
+                    stop=False,
+                )
+
+        mix_shared(c_mix[1], c_second, S)
+        c_codes.append(held([P, S], U32, "c_codes1"))
+        quantise(c_codes[1][:], c_scale[1][:], c_mix[1][:])
+
+        for piece, (lo, hi) in enumerate(U_PIECES):
+            for a in range(NC):
+                if piece == 0 and a == NC - 1:
+                    mix_shared(u_mix[a][:, lo:hi, :], u_raw[piece][a], hi - lo)
+                else:
+                    mix(piece < 2, u_mix[a][:, lo:hi, :], u_raw[piece][a][:])
+                quantise(u_codes[a][:, lo:hi], u_scale[a][:, lo:hi], u_mix[a][:, lo:hi, :])
+            for m in range(lo // P, hi // P):
+                cols = slice(P * m, P * (m + 1))
+                for a in range(NC):
+                    nc.tensor.matmul_mx(
+                        out=sums[m][:],
+                        lhsT=u_codes[a][:, cols].bitcast(FP8X4),
+                        lhsT_scale=u_scale[a][:, cols],
+                        rhs=c_codes[a][:].bitcast(FP8X4),
+                        rhs_scale=c_scale[a][:],
+                        start=False,
+                        stop=a == NC - 1,
+                    )
+                finish(m, 2 if m == NM - 1 else 1)

@@ -37,6 +37,9 @@ def tile_list_hmix_gelu_kernel(tc, xT, w4_words, w4_scales, c, u, wgt, b, offs, 
         offsets = keep.tile([P, S // 16], U16, name="offsets")
         weight_all = held([P, S], F32, "weight_all")
         weight = [weight_all[:, 0:H], weight_all[:, H:S]]
+        w_dealt = held([P, 32], F32, "w_dealt")
+        w_turned = held([P, 32], F32, "w_turned")
+        w_spread = held([P, S], F32, "w_spread")
         planes = [[held([P, T], F32, "plane%d_%d" % (a, i)) for i in range(4)] for a in range(NX)]
         picked = [held([P, 4, S], F32, "picked%d" % a) for a in range(NX)]
         c_first = [held([P, 4, H], F32, "c_first%d" % h) for h in range(2)]
@@ -92,14 +95,18 @@ def tile_list_hmix_gelu_kernel(tc, xT, w4_words, w4_scales, c, u, wgt, b, offs, 
         make_identity(nc, ident[:])
         nc.scalar.activation(warm[:], warm[:], GELU)
 
+        nc.sync.dma_start(w_dealt[:], wgt.rearrange("(g r) (c y) -> g r c y", r=16, y=32)[:, 0, :, :])
         nc.sync.dma_start(offsets[:], offs)
-        nc.sync.dma_start(weight[0], wgt[:, 0:H])
+        nc.vector.transpose(w_turned[:], w_dealt[:])
+        nc.vector.tensor_copy(
+            w_spread[:].rearrange("p (c h r) -> p c h r", h=2, r=16),
+            w_turned[:].rearrange("p (h c) -> p c h", h=2).unsqueeze(3).to_broadcast([P, 16, 2, 16]),
+        )
+        nc.vector.transpose(weight_all[:], w_spread[:])
         for a in range(NX):
             rows = xT[KP * a : KP * (a + 1), :].rearrange("(p i) t -> p i t", i=4)
             for i in range(4):
                 nc.sync.dma_start(planes[a][i][:], rows[:, i, :])
-                if a == 0 and i == 0:
-                    nc.sync.dma_start(weight[1], wgt[:, H:S])
                 if a > 0 and i == 1:
                     load_rows(c_first[a - 1], c, 0, H * (a - 1), H * a)
                 if a == 1:
@@ -118,7 +125,7 @@ def tile_list_hmix_gelu_kernel(tc, xT, w4_words, w4_scales, c, u, wgt, b, offs, 
         x_codes, c_codes = [], []
         for a in range(NX):
             for i in range(4):
-                if (a, i) in ((0, 0), (NX - 1, 3)):
+                if (a, i) == (NX - 1, 3):
                     for h in range(2):
                         listed = offsets[:, h * H // 16 : (h + 1) * H // 16]
                         cols = slice(h * H, (h + 1) * H)

@@ -22,6 +22,8 @@ KP = 512
 NX, NC = K // KP, L // KP
 NM = M // P
 H = S // 2
+U_ON_SCALAR = ((1, 1), (2, 0), (2, 1))
+C_PIECES = {(1, 1): (0, 0, S), (2, 1): (1, 0, H), (2, 2): (1, H, S)}
 U_PIECES = ((0, 2 * P), (2 * P, 3 * P), (3 * P, 4 * P))
 
 
@@ -35,24 +37,24 @@ def tile_list_hmix_gelu_kernel(tc, xT, w4_words, w4_scales, c, u, wgt, b, offs, 
             return keep.tile(shape, dtype, name=name, tag=tag or name, align_bytes=64)
 
         offsets = keep.tile([P, S // 16], U16, name="offsets")
-        weight_all = held([P, S], F32, "weight_all")
-        weight = [weight_all[:, 0:H], weight_all[:, H:S]]
         w_dealt = held([P, 32], F32, "w_dealt")
         w_turned = held([P, 32], F32, "w_turned")
         w_spread = held([P, S], F32, "w_spread")
+        weight = held([P, S], F32, "weight")
         planes = [[held([P, T], F32, "plane%d_%d" % (a, i)) for i in range(4)] for a in range(NX)]
         picked = [held([P, 4, S], F32, "picked%d" % a) for a in range(NX)]
-        c_first = [held([P, 4, H], F32, "c_first%d" % h) for h in range(2)]
-        c_second = held([P, 4, S], F32, "c_second")
+        c_raw = {key: held([P, 4, C_PIECES[key][2] - C_PIECES[key][1]], F32, "c_raw%d_%d" % key) for key in C_PIECES}
         u_raw = [[held([P, 4, hi - lo], F32, "u_raw%d_%d" % (a, lo)) for a in range(NC)] for lo, hi in U_PIECES]
-        x_mix = [held([P, S, 4], BF16, "x_mix%d" % a) for a in range(NX)]
-        c_mix = [held([P, S, 4], BF16, "c_mix%d" % a) for a in range(NC)]
-        u_mix = [held([P, M, 4], BF16, "u_mix%d" % a) for a in range(NC)]
-        u_codes = [held([P, M], U32, "u_codes%d" % a) for a in range(NC)]
-        x_scale = [held([P, S], U8, "x_scale%d" % a) for a in range(NX)]
-        c_scale = [held([P, S], U8, "c_scale%d" % a) for a in range(NC)]
-        u_scale = [held([P, M], U8, "u_scale%d" % a) for a in range(NC)]
-        w_words = held([P, NX, 2 * M], U8, "w_words")
+        mixed = [held([P, S * (1 + min(a, 1)), 4], BF16, "mixed%d" % a) for a in range(NX)]
+        scales = [held([P, S * (1 + min(a, 1))], U8, "scales%d" % a) for a in range(NX)]
+        x_mix = [tile[:, 0:S, :] for tile in mixed]
+        c_mix = [tile[:, S : 2 * S, :] for tile in mixed[1:]]
+        u_mix = [held([P, NC, P, 4], BF16, "u_mix%d" % m) for m in range(NM)]
+        u_codes = [held([P, NC, P], U32, "u_codes%d" % m) for m in range(NM)]
+        u_scale = [held([P, NC, P], U8, "u_scale%d" % m) for m in range(NM)]
+        w_first = held([P, 2 * M], U8, "w_first")
+        w_rest = held([P, NX - 1, 2 * M], U8, "w_rest")
+        w_words = [w_first[:]] + [w_rest[:, a, :] for a in range(NX - 1)]
         w_scale = held([P, NX, M], U8, "w_scale")
         b_rows = held([P, P], F32, "b_rows")
         b_cols = held([P, NM], F32, "b_cols")
@@ -74,13 +76,23 @@ def tile_list_hmix_gelu_kernel(tc, xT, w4_words, w4_scales, c, u, wgt, b, offs, 
             else:
                 nc.vector.tensor_copy(dst, src)
 
-        def mix_shared(dst, src, width):
-            half = width // 2
-            mix(False, dst[:, 0:half, :], src[:, :, 0:half])
-            mix(True, dst[:, half:width, :], src[:, :, half:width])
+        def quantise(words, scale, values):
+            nc.vector.quantize_mx(out=words.bitcast(FP8X4), scales=scale, in_=values.rearrange("p w i -> p (w i)"))
 
-        def quantise(codes, scale, mixed):
-            nc.vector.quantize_mx(out=codes.bitcast(FP8X4), scales=scale, in_=mixed.rearrange("p w i -> p (w i)"))
+        def gather(a, i, lo, hi):
+            listed = offsets[:, lo // 16 : hi // 16]
+            nc.vector.tensor_tensor(picked[a][:, i, lo:hi], planes[a][i][:].indirect(listed), weight[:, lo:hi], MULT)
+
+        def times_w4(a, m):
+            nc.tensor.matmul_mx(
+                out=sums[m][:],
+                lhsT=w_words[a][:, 2 * P * m : 2 * P * (m + 1)].bitcast(FP4X4),
+                lhsT_scale=w_scale[:, a, P * m : P * (m + 1)],
+                rhs=codes[a][:, 0:S].bitcast(FP8X4),
+                rhs_scale=scales[a][:, 0:S],
+                start=a == 0,
+                stop=False,
+            )
 
         def finish(m, pieces):
             width = S // pieces
@@ -94,95 +106,89 @@ def tile_list_hmix_gelu_kernel(tc, xT, w4_words, w4_scales, c, u, wgt, b, offs, 
         nc.gpsimd.memset(warm[:], 0.0)
         make_identity(nc, ident[:])
         nc.scalar.activation(warm[:], warm[:], GELU)
+        for q in range(4):
+            nc.gpsimd.dma_start(
+                w_scale[32 * q : 32 * q + 4, :, :].bitcast(I32),
+                w4_scales[:, 4 * q : 4 * q + 4, :].rearrange("a r n -> r a n").bitcast(I32),
+            )
 
         nc.sync.dma_start(w_dealt[:], wgt.rearrange("(g r) (c y) -> g r c y", r=16, y=32)[:, 0, :, :])
         nc.sync.dma_start(offsets[:], offs)
+        for a in range(NX):
+            rows = xT[KP * a : KP * (a + 1), :].rearrange("(p i) t -> p i t", i=4)
+            for i in range(4):
+                nc.sync.dma_start(planes[a][i][:], rows[:, i, :])
+                if (a, i) in C_PIECES:
+                    load_rows(c_raw[a, i], c, *C_PIECES[a, i])
+                if (a, i) == (1, 3):
+                    nc.sync.dma_start(w_first[:].bitcast(I32), w4_words[0].bitcast(I32))
+        nc.sync.dma_start(b_rows[0:NM, :], b.rearrange("(m p) -> m p", p=P))
+        nc.sync.dma_start(w_rest[:], w4_words[1:NX].rearrange("a p n -> p a n"))
+        for piece, (lo, hi) in enumerate(U_PIECES):
+            for a in range(NC):
+                load_rows(u_raw[piece][a], u, a, lo, hi)
+
         nc.vector.transpose(w_turned[:], w_dealt[:])
         nc.vector.tensor_copy(
             w_spread[:].rearrange("p (c h r) -> p c h r", h=2, r=16),
             w_turned[:].rearrange("p (h c) -> p c h", h=2).unsqueeze(3).to_broadcast([P, 16, 2, 16]),
         )
-        nc.vector.transpose(weight_all[:], w_spread[:])
-        for a in range(NX):
-            rows = xT[KP * a : KP * (a + 1), :].rearrange("(p i) t -> p i t", i=4)
-            for i in range(4):
-                nc.sync.dma_start(planes[a][i][:], rows[:, i, :])
-                if a > 0 and i == 1:
-                    load_rows(c_first[a - 1], c, 0, H * (a - 1), H * a)
-                if a == 1:
-                    nc.sync.dma_start(
-                        w_scale[32 * i : 32 * i + 4, :, :].bitcast(I32),
-                        w4_scales[:, 4 * i : 4 * i + 4, :].rearrange("a r n -> r a n").bitcast(I32),
-                    )
-                if a == NX - 1 and i == 2:
-                    nc.sync.dma_start(b_rows[0:NM, :], b.rearrange("(m p) -> m p", p=P))
-                    nc.sync.dma_start(w_words[:], w4_words.rearrange("a p n -> p a n"))
-        load_rows(c_second, c, 1, 0, S)
-        for piece, (lo, hi) in enumerate(U_PIECES):
-            for a in range(NC):
-                load_rows(u_raw[piece][a], u, a, lo, hi)
+        nc.vector.transpose(weight[:], w_spread[:])
 
-        x_codes, c_codes = [], []
+        codes = []
+        last = NX - 1
         for a in range(NX):
             for i in range(4):
-                if (a, i) == (NX - 1, 3):
-                    for h in range(2):
-                        listed = offsets[:, h * H // 16 : (h + 1) * H // 16]
-                        cols = slice(h * H, (h + 1) * H)
-                        nc.vector.tensor_tensor(picked[a][:, i, cols], planes[a][i][:].indirect(listed), weight[h], MULT)
+                if (a, i) == (last, 3):
+                    gather(a, i, 0, H)
+                    gather(a, i, H, S)
                 else:
-                    nc.vector.tensor_tensor(
-                        picked[a][:, i, :], planes[a][i][:].indirect(offsets[:]), weight_all[:], MULT
-                    )
+                    gather(a, i, 0, S)
+                if (a, i) in C_PIECES:
+                    n, lo, hi = C_PIECES[a, i]
+                    mix(True, c_mix[n][:, lo:hi, :], c_raw[a, i][:])
                 if a > 0 and i == 1:
-                    x_codes.append(held([P, S], U32, "x_codes%d" % (a - 1), "plane%d_1" % a))
-                    quantise(x_codes[a - 1][:], x_scale[a - 1][:], x_mix[a - 1][:])
-                    mix(True, c_mix[0][:, H * (a - 1) : H * a, :], c_first[a - 1][:])
-                if a == NX - 1 and i == 2:
-                    c_codes.append(held([P, S], U32, "c_codes0", "plane%d_2" % a))
-                    quantise(c_codes[0][:], c_scale[0][:], c_mix[0][:])
-            if a < NX - 1:
-                mix(True, x_mix[a][:], picked[a][:])
-        mix(True, x_mix[NX - 1][:, 0:H, :], picked[NX - 1][:, :, 0:H])
-        mix(False, x_mix[NX - 1][:, H:S, :], picked[NX - 1][:, :, H:S])
-        x_codes.append(held([P, S], U32, "x_codes2"))
-        quantise(x_codes[NX - 1][:], x_scale[NX - 1][:], x_mix[NX - 1][:])
-
+                    codes.append(held([P, S * a], U32, "codes%d" % (a - 1), "plane%d_1" % a))
+                    quantise(codes[a - 1][:], scales[a - 1][:], mixed[a - 1][:])
+            if a < last:
+                mix(True, x_mix[a], picked[a][:])
+        mix(True, x_mix[last][:, 0:H, :], picked[last][:, :, 0:H])
+        mix(False, x_mix[last][:, H:S, :], picked[last][:, :, H:S])
         nc.tensor.transpose(b_turned[:], b_rows[:], ident[:])
         nc.scalar.copy(b_cols[:], b_turned[:, 0:NM])
+        codes.append(held([P, 2 * S], U32, "codes%d" % last))
+        for cols in (slice(0, S), slice(S, 2 * S)):
+            quantise(codes[last][:, cols], scales[last][:, cols], mixed[last][:, cols, :])
 
-        for a in range(NX):
+        for a in range(last):
             for m in range(NM):
-                nc.tensor.matmul_mx(
-                    out=sums[m][:],
-                    lhsT=w_words[:, a, 2 * P * m : 2 * P * (m + 1)].bitcast(FP4X4),
-                    lhsT_scale=w_scale[:, a, P * m : P * (m + 1)],
-                    rhs=x_codes[a][:].bitcast(FP8X4),
-                    rhs_scale=x_scale[a][:],
-                    start=a == 0,
-                    stop=False,
-                )
+                times_w4(a, m)
 
-        mix_shared(c_mix[1], c_second, S)
-        c_codes.append(held([P, S], U32, "c_codes1"))
-        quantise(c_codes[1][:], c_scale[1][:], c_mix[1][:])
-
+        mix(True, u_mix[0][:, 0, :, :], u_raw[0][0][:, :, 0:P])
+        mix(True, u_mix[1][:, 0, :, :], u_raw[0][0][:, :, P : 2 * P])
         for piece, (lo, hi) in enumerate(U_PIECES):
-            for a in range(NC):
-                if piece == 0 and a == NC - 1:
-                    mix_shared(u_mix[a][:, lo:hi, :], u_raw[piece][a], hi - lo)
-                else:
-                    mix(piece < 2, u_mix[a][:, lo:hi, :], u_raw[piece][a][:])
-                quantise(u_codes[a][:, lo:hi], u_scale[a][:, lo:hi], u_mix[a][:, lo:hi, :])
             for m in range(lo // P, hi // P):
-                cols = slice(P * m, P * (m + 1))
+                cols = slice(P * m - lo, P * (m + 1) - lo)
+                for a in range(NC):
+                    if (piece, a) != (0, 0):
+                        mix((m, a) in U_ON_SCALAR, u_mix[m][:, a, :, :], u_raw[piece][a][:, :, cols])
+                if m < NM - 1:
+                    quantise(
+                        u_codes[m][:].rearrange("p a n -> p (a n)"),
+                        u_scale[m][:].rearrange("p a n -> p (a n)"),
+                        u_mix[m][:].rearrange("p a n i -> p (a n) i"),
+                    )
+                else:
+                    for a in range(NC):
+                        quantise(u_codes[m][:, a, :], u_scale[m][:, a, :], u_mix[m][:, a, :, :])
+                times_w4(last, m)
                 for a in range(NC):
                     nc.tensor.matmul_mx(
                         out=sums[m][:],
-                        lhsT=u_codes[a][:, cols].bitcast(FP8X4),
-                        lhsT_scale=u_scale[a][:, cols],
-                        rhs=c_codes[a][:].bitcast(FP8X4),
-                        rhs_scale=c_scale[a][:],
+                        lhsT=u_codes[m][:, a, :].bitcast(FP8X4),
+                        lhsT_scale=u_scale[m][:, a, :],
+                        rhs=codes[a + 1][:, S : 2 * S].bitcast(FP8X4),
+                        rhs_scale=scales[a + 1][:, S : 2 * S],
                         start=False,
                         stop=a == NC - 1,
                     )

@@ -22,8 +22,7 @@ KP = 512
 NX, NC = K // KP, L // KP
 NM = M // P
 H = S // 2
-U_ON_SCALAR = ((1, 1), (2, 0), (2, 1))
-C_PIECES = {(1, 1): (0, 0, S), (2, 1): (1, 0, H), (2, 2): (1, H, S)}
+
 U_PIECES = ((0, 2 * P), (2 * P, 3 * P), (3 * P, 4 * P))
 
 
@@ -43,15 +42,16 @@ def tile_list_hmix_gelu_kernel(tc, xT, w4_words, w4_scales, c, u, wgt, b, offs, 
         weight = held([P, S], F32, "weight")
         planes = [[held([P, T], F32, "plane%d_%d" % (a, i)) for i in range(4)] for a in range(NX)]
         picked = [held([P, 4, S], F32, "picked%d" % a) for a in range(NX)]
-        c_raw = {key: held([P, 4, C_PIECES[key][2] - C_PIECES[key][1]], F32, "c_raw%d_%d" % key) for key in C_PIECES}
-        u_raw = [[held([P, 4, hi - lo], F32, "u_raw%d_%d" % (a, lo)) for a in range(NC)] for lo, hi in U_PIECES]
+        c_raw = [held([P, 4, S], F32, "c_raw%d" % a) for a in range(NC)]
+        u_first = held([P, 4, M], F32, "u_first")
+        u_last = [held([P, 4, hi - lo], F32, "u_last%d" % lo) for lo, hi in U_PIECES]
         mixed = [held([P, S * (1 + min(a, 1)), 4], BF16, "mixed%d" % a) for a in range(NX)]
         scales = [held([P, S * (1 + min(a, 1))], U8, "scales%d" % a) for a in range(NX)]
         x_mix = [tile[:, 0:S, :] for tile in mixed]
         c_mix = [tile[:, S : 2 * S, :] for tile in mixed[1:]]
-        u_mix = [held([P, NC, P, 4], BF16, "u_mix%d" % m) for m in range(NM)]
-        u_codes = [held([P, NC, P], U32, "u_codes%d" % m) for m in range(NM)]
-        u_scale = [held([P, NC, P], U8, "u_scale%d" % m) for m in range(NM)]
+        u_mix = [held([P, M, 4], BF16, "u_mix%d" % a) for a in range(NC)]
+        u_codes = [held([P, M], U32, "u_codes%d" % a) for a in range(NC)]
+        u_scale = [held([P, M], U8, "u_scale%d" % a) for a in range(NC)]
         w_first = held([P, 2 * M], U8, "w_first")
         w_rest = held([P, NX - 1, 2 * M], U8, "w_rest")
         w_words = [w_first[:]] + [w_rest[:, a, :] for a in range(NX - 1)]
@@ -106,27 +106,27 @@ def tile_list_hmix_gelu_kernel(tc, xT, w4_words, w4_scales, c, u, wgt, b, offs, 
         nc.gpsimd.memset(warm[:], 0.0)
         make_identity(nc, ident[:])
         nc.scalar.activation(warm[:], warm[:], GELU)
-        for q in range(4):
-            nc.gpsimd.dma_start(
-                w_scale[32 * q : 32 * q + 4, :, :].bitcast(I32),
-                w4_scales[:, 4 * q : 4 * q + 4, :].rearrange("a r n -> r a n").bitcast(I32),
-            )
 
-        nc.sync.dma_start(w_dealt[:], wgt.rearrange("(g r) (c y) -> g r c y", r=16, y=32)[:, 0, :, :])
+        nc.sync.dma_start(w_dealt[:], wgt.rearrange("r (h w) -> (r h) w", h=2)[0 : 2 * P : 17, :])
         nc.sync.dma_start(offsets[:], offs)
         for a in range(NX):
             rows = xT[KP * a : KP * (a + 1), :].rearrange("(p i) t -> p i t", i=4)
             for i in range(4):
                 nc.sync.dma_start(planes[a][i][:], rows[:, i, :])
-                if (a, i) in C_PIECES:
-                    load_rows(c_raw[a, i], c, *C_PIECES[a, i])
+                if a > 0 and i == 1:
+                    load_rows(c_raw[a - 1], c, a - 1, 0, S)
+                if a == 1:
+                    nc.sync.dma_start(
+                        w_scale[32 * i : 32 * i + 4, :, :].bitcast(I32),
+                        w4_scales[:, 4 * i : 4 * i + 4, :].rearrange("a r n -> r a n").bitcast(I32),
+                    )
                 if (a, i) == (1, 3):
                     nc.sync.dma_start(w_first[:].bitcast(I32), w4_words[0].bitcast(I32))
         nc.sync.dma_start(b_rows[0:NM, :], b.rearrange("(m p) -> m p", p=P))
         nc.sync.dma_start(w_rest[:], w4_words[1:NX].rearrange("a p n -> p a n"))
+        load_rows(u_first, u, 0, 0, M)
         for piece, (lo, hi) in enumerate(U_PIECES):
-            for a in range(NC):
-                load_rows(u_raw[piece][a], u, a, lo, hi)
+            load_rows(u_last[piece], u, 1, lo, hi)
 
         nc.vector.transpose(w_turned[:], w_dealt[:])
         nc.vector.tensor_copy(
@@ -144,9 +144,8 @@ def tile_list_hmix_gelu_kernel(tc, xT, w4_words, w4_scales, c, u, wgt, b, offs, 
                     gather(a, i, H, S)
                 else:
                     gather(a, i, 0, S)
-                if (a, i) in C_PIECES:
-                    n, lo, hi = C_PIECES[a, i]
-                    mix(True, c_mix[n][:, lo:hi, :], c_raw[a, i][:])
+                if a > 0 and i == 1:
+                    mix(True, c_mix[a - 1], c_raw[a - 1][:])
                 if a > 0 and i == 1:
                     codes.append(held([P, S * a], U32, "codes%d" % (a - 1), "plane%d_1" % a))
                     quantise(codes[a - 1][:], scales[a - 1][:], mixed[a - 1][:])
@@ -156,7 +155,7 @@ def tile_list_hmix_gelu_kernel(tc, xT, w4_words, w4_scales, c, u, wgt, b, offs, 
         mix(False, x_mix[last][:, H:S, :], picked[last][:, :, H:S])
         nc.tensor.transpose(b_turned[:], b_rows[:], ident[:])
         nc.scalar.copy(b_cols[:], b_turned[:, 0:NM])
-        codes.append(held([P, 2 * S], U32, "codes%d" % last))
+        codes.append(held([P, 2 * S], U32, "codes%d" % last, "plane%d_3" % last))
         for cols in (slice(0, S), slice(S, 2 * S)):
             quantise(codes[last][:, cols], scales[last][:, cols], mixed[last][:, cols, :])
 
@@ -164,29 +163,28 @@ def tile_list_hmix_gelu_kernel(tc, xT, w4_words, w4_scales, c, u, wgt, b, offs, 
             for m in range(NM):
                 times_w4(a, m)
 
-        mix(True, u_mix[0][:, 0, :, :], u_raw[0][0][:, :, 0:P])
-        mix(True, u_mix[1][:, 0, :, :], u_raw[0][0][:, :, P : 2 * P])
+        def mix_u(a, raw, lo, hi, on_scalar):
+            mix(on_scalar, u_mix[a][:, lo:hi, :], raw)
+
+        def quantise_u(a, lo, hi):
+            quantise(u_codes[a][:, lo:hi], u_scale[a][:, lo:hi], u_mix[a][:, lo:hi, :])
+
+        mix_u(0, u_first[:, :, 0 : 2 * P], 0, 2 * P, True)
+        mix_u(0, u_first[:, :, 2 * P : M], 2 * P, M, True)
+        quantise_u(0, 0, 2 * P)
         for piece, (lo, hi) in enumerate(U_PIECES):
             for m in range(lo // P, hi // P):
-                cols = slice(P * m - lo, P * (m + 1) - lo)
-                for a in range(NC):
-                    if (piece, a) != (0, 0):
-                        mix((m, a) in U_ON_SCALAR, u_mix[m][:, a, :, :], u_raw[piece][a][:, :, cols])
-                if m < NM - 1:
-                    quantise(
-                        u_codes[m][:].rearrange("p a n -> p (a n)"),
-                        u_scale[m][:].rearrange("p a n -> p (a n)"),
-                        u_mix[m][:].rearrange("p a n i -> p (a n) i"),
-                    )
-                else:
-                    for a in range(NC):
-                        quantise(u_codes[m][:, a, :], u_scale[m][:, a, :], u_mix[m][:, a, :, :])
+                cols = slice(P * m, P * (m + 1))
+                mix_u(1, u_last[piece][:, :, P * m - lo : P * (m + 1) - lo], P * m, P * (m + 1), m == 1)
+                quantise_u(1, P * m, P * (m + 1))
+                if m == 0:
+                    quantise_u(0, 2 * P, M)
                 times_w4(last, m)
                 for a in range(NC):
                     nc.tensor.matmul_mx(
                         out=sums[m][:],
-                        lhsT=u_codes[m][:, a, :].bitcast(FP8X4),
-                        lhsT_scale=u_scale[m][:, a, :],
+                        lhsT=u_codes[a][:, cols].bitcast(FP8X4),
+                        lhsT_scale=u_scale[a][:, cols],
                         rhs=codes[a + 1][:, S : 2 * S].bitcast(FP8X4),
                         rhs_scale=scales[a + 1][:, S : 2 * S],
                         start=False,

@@ -61,7 +61,8 @@ def tile_list_hmix_gelu_kernel(tc, xT, w4_words, w4_scales, c, u, wgt, b, offs, 
         ident = held([P, P], F32, "ident")
         warm = held([P, 1], F32, "warm")
         result = [held([P, S], F32, "result%d" % m) for m in range(NM)]
-        sums = [psum.tile([P, S], F32, name="sums%d" % m, tag="sums%d" % m) for m in range(NM)]
+        parts = [(m, 0, S) for m in range(NM - 1)] + [(NM - 1, 0, H), (NM - 1, H, S)]
+        sums = {part: psum.tile([P, part[2] - part[1]], F32, name="sums%d_%d" % part[:2]) for part in parts}
         b_turned = psum.tile([P, P], F32, name="b_turned")
 
         def load_rows(tile, src, a, lo, hi):
@@ -83,23 +84,36 @@ def tile_list_hmix_gelu_kernel(tc, xT, w4_words, w4_scales, c, u, wgt, b, offs, 
             listed = offsets[:, lo // 16 : hi // 16]
             nc.vector.tensor_tensor(picked[a][:, i, lo:hi], planes[a][i][:].indirect(listed), weight[:, lo:hi], MULT)
 
-        def times_w4(a, m):
+        def times_w4(a, part):
+            m, lo, hi = part
+            width = S if hi - lo == S else P
+            for at in range(lo, hi, width):
+                nc.tensor.matmul_mx(
+                    out=sums[part][:, at - lo : at - lo + width],
+                    lhsT=w_words[a][:, 2 * P * m : 2 * P * (m + 1)].bitcast(FP4X4),
+                    lhsT_scale=w_scale[:, a, P * m : P * (m + 1)],
+                    rhs=codes[a][:, at : at + width].bitcast(FP8X4),
+                    rhs_scale=scales[a][:, at : at + width],
+                    start=a == 0 and at == lo,
+                    stop=False,
+                )
+
+        def times_u(a, part):
+            m, lo, hi = part
             nc.tensor.matmul_mx(
-                out=sums[m][:],
-                lhsT=w_words[a][:, 2 * P * m : 2 * P * (m + 1)].bitcast(FP4X4),
-                lhsT_scale=w_scale[:, a, P * m : P * (m + 1)],
-                rhs=codes[a][:, 0:S].bitcast(FP8X4),
-                rhs_scale=scales[a][:, 0:S],
-                start=a == 0,
-                stop=False,
+                out=sums[part][:],
+                lhsT=u_codes[a][:, P * m : P * (m + 1)].bitcast(FP8X4),
+                lhsT_scale=u_scale[a][:, P * m : P * (m + 1)],
+                rhs=codes[a + 1][:, S + lo : S + hi].bitcast(FP8X4),
+                rhs_scale=scales[a + 1][:, S + lo : S + hi],
+                start=False,
+                stop=a == NC - 1,
             )
 
-        def finish(m, pieces):
-            width = S // pieces
-            for j in range(pieces):
-                cols = slice(width * j, width * (j + 1))
-                nc.scalar.activation(result[m][:, cols], sums[m][:, cols], GELU, bias=b_cols[:, m : m + 1])
-                nc.sync.dma_start(out[P * m : P * (m + 1), cols], result[m][:, cols])
+        def finish(part):
+            m, lo, hi = part
+            nc.scalar.activation(result[m][:, lo:hi], sums[part][:], GELU, bias=b_cols[:, m : m + 1])
+            nc.sync.dma_start(out[P * m : P * (m + 1), lo:hi], result[m][:, lo:hi])
 
         nc.gpsimd.memset(w_scale[:].rearrange("p a n -> p (a n)").bitcast(I32), 0)
         nc.gpsimd.memset(b_rows[:], 0.0)
@@ -160,8 +174,8 @@ def tile_list_hmix_gelu_kernel(tc, xT, w4_words, w4_scales, c, u, wgt, b, offs, 
             quantise(codes[last][:, cols], scales[last][:, cols], mixed[last][:, cols, :])
 
         for a in range(last):
-            for m in range(NM):
-                times_w4(a, m)
+            for part in parts:
+                times_w4(a, part)
 
         def mix_u(a, raw, lo, hi, on_scalar):
             mix(on_scalar, u_mix[a][:, lo:hi, :], raw)
@@ -169,7 +183,8 @@ def tile_list_hmix_gelu_kernel(tc, xT, w4_words, w4_scales, c, u, wgt, b, offs, 
         def quantise_u(a, lo, hi):
             quantise(u_codes[a][:, lo:hi], u_scale[a][:, lo:hi], u_mix[a][:, lo:hi, :])
 
-        mix_u(0, u_first[:, :, 0 : 2 * P], 0, 2 * P, True)
+        mix_u(0, u_first[:, :, 0:P], 0, P, False)
+        mix_u(0, u_first[:, :, P : 2 * P], P, 2 * P, True)
         mix_u(0, u_first[:, :, 2 * P : M], 2 * P, M, True)
         quantise_u(0, 0, 2 * P)
         for piece, (lo, hi) in enumerate(U_PIECES):
@@ -179,15 +194,8 @@ def tile_list_hmix_gelu_kernel(tc, xT, w4_words, w4_scales, c, u, wgt, b, offs, 
                 quantise_u(1, P * m, P * (m + 1))
                 if m == 0:
                     quantise_u(0, 2 * P, M)
-                times_w4(last, m)
-                for a in range(NC):
-                    nc.tensor.matmul_mx(
-                        out=sums[m][:],
-                        lhsT=u_codes[a][:, cols].bitcast(FP8X4),
-                        lhsT_scale=u_scale[a][:, cols],
-                        rhs=codes[a + 1][:, S : 2 * S].bitcast(FP8X4),
-                        rhs_scale=scales[a + 1][:, S : 2 * S],
-                        start=False,
-                        stop=a == NC - 1,
-                    )
-                finish(m, 2 if m == NM - 1 else 1)
+                for part in [part for part in parts if part[0] == m]:
+                    times_w4(last, part)
+                    for a in range(NC):
+                        times_u(a, part)
+                    finish(part)

@@ -131,8 +131,8 @@ def tile_list_hmix_gelu_kernel(tc, xT, w4_words, w4_scales, c, u, wgt, b, offs, 
                     load_rows(c_raw[a - 1], c, a - 1, 0, S)
                 if a == 1:
                     nc.sync.dma_start(
-                        w_scale[32 * i : 32 * i + 4, :, :].bitcast(I32),
-                        w4_scales[:, 4 * i : 4 * i + 4, :].rearrange("a r n -> r a n").bitcast(I32),
+                        w_scale[i:P:32, :, :].bitcast(I32),
+                        w4_scales[:, i:16:4, :].rearrange("a q n -> q a n").bitcast(I32),
                     )
                 if (a, i) == (1, 3):
                     nc.sync.dma_start(w_first[:].bitcast(I32), w4_words[0].bitcast(I32))

@@ -49,9 +49,10 @@ def tile_list_hmix_gelu_kernel(tc, xT, w4_words, w4_scales, c, u, wgt, b, offs, 
         scales = [held([P, S * (1 + min(a, 1))], U8, "scales%d" % a) for a in range(NX)]
         x_mix = [tile[:, 0:S, :] for tile in mixed]
         c_mix = [tile[:, S : 2 * S, :] for tile in mixed[1:]]
-        u_mix = [held([P, M, 4], BF16, "u_mix%d" % a) for a in range(NC)]
-        u_codes = [held([P, M], U32, "u_codes%d" % a) for a in range(NC)]
+        u_mix = held([P, M, 4], BF16, "u_mix")
+        u_codes = held([P, M], U32, "u_codes")
         u_scale = [held([P, M], U8, "u_scale%d" % a) for a in range(NC)]
+        last_codes = {}
         w_first = held([P, 2 * M], U8, "w_first")
         w_rest = held([P, NX - 1, 2 * M], U8, "w_rest")
         w_words = [w_first[:]] + [w_rest[:, a, :] for a in range(NX - 1)]
@@ -102,7 +103,7 @@ def tile_list_hmix_gelu_kernel(tc, xT, w4_words, w4_scales, c, u, wgt, b, offs, 
             m, lo, hi = part
             nc.tensor.matmul_mx(
                 out=sums[part][:],
-                lhsT=u_codes[a][:, P * m : P * (m + 1)].bitcast(FP8X4),
+                lhsT=(last_codes[m][:] if a == NC - 1 else u_codes[:, P * m : P * (m + 1)]).bitcast(FP8X4),
                 lhsT_scale=u_scale[a][:, P * m : P * (m + 1)],
                 rhs=codes[a + 1][:, S + lo : S + hi].bitcast(FP8X4),
                 rhs_scale=scales[a + 1][:, S + lo : S + hi],
@@ -136,7 +137,8 @@ def tile_list_hmix_gelu_kernel(tc, xT, w4_words, w4_scales, c, u, wgt, b, offs, 
                     )
                 if (a, i) == (1, 3):
                     nc.sync.dma_start(w_first[:].bitcast(I32), w4_words[0].bitcast(I32))
-        nc.sync.dma_start(b_rows[0:NM, :], b.rearrange("(m p) -> m p", p=P))
+                if (a, i) == (0, 3):
+                    nc.sync.dma_start(b_rows[0:NM, :], b.rearrange("(m p) -> m p", p=P))
         nc.sync.dma_start(w_rest[:], w4_words[1:NX].rearrange("a p n -> p a n"))
         load_rows(u_first, u, 0, 0, M)
         for piece, (lo, hi) in enumerate(U_PIECES):
@@ -158,6 +160,8 @@ def tile_list_hmix_gelu_kernel(tc, xT, w4_words, w4_scales, c, u, wgt, b, offs, 
                     gather(a, i, H, S)
                 else:
                     gather(a, i, 0, S)
+                if (a, i) == (last, 1):
+                    mix(True, x_mix[a][:, :, 0:2], picked[a][:, 0:2, :])
                 if a > 0 and i == 1:
                     mix(True, c_mix[a - 1], c_raw[a - 1][:])
                 if a > 0 and i == 1:
@@ -165,8 +169,8 @@ def tile_list_hmix_gelu_kernel(tc, xT, w4_words, w4_scales, c, u, wgt, b, offs, 
                     quantise(codes[a - 1][:], scales[a - 1][:], mixed[a - 1][:])
             if a < last:
                 mix(True, x_mix[a], picked[a][:])
-        mix(True, x_mix[last][:, 0:H, :], picked[last][:, :, 0:H])
-        mix(False, x_mix[last][:, H:S, :], picked[last][:, :, H:S])
+        mix(True, x_mix[last][:, 0:H, 2:4], picked[last][:, 2:4, 0:H])
+        mix(False, x_mix[last][:, H:S, 2:4], picked[last][:, 2:4, H:S])
         nc.tensor.transpose(b_turned[:], b_rows[:], ident[:])
         nc.scalar.copy(b_cols[:], b_turned[:, 0:NM])
         codes.append(held([P, 2 * S], U32, "codes%d" % last, "plane%d_3" % last))
@@ -177,25 +181,45 @@ def tile_list_hmix_gelu_kernel(tc, xT, w4_words, w4_scales, c, u, wgt, b, offs, 
             for part in parts:
                 times_w4(a, part)
 
-        def mix_u(a, raw, lo, hi, on_scalar):
-            mix(on_scalar, u_mix[a][:, lo:hi, :], raw)
+        def mix_first(lo, hi, on_scalar):
+            mix(on_scalar, u_mix[:, P * lo : P * hi, :], u_first[:, :, P * lo : P * hi])
 
-        def quantise_u(a, lo, hi):
-            quantise(u_codes[a][:, lo:hi], u_scale[a][:, lo:hi], u_mix[a][:, lo:hi, :])
+        def first_pass(lo, hi):
+            cols = slice(P * lo, P * hi)
+            quantise(u_codes[:, cols], u_scale[0][:, cols], u_mix[:, cols, :])
+            for part in parts:
+                if lo <= part[0] < hi:
+                    times_u(0, part)
 
-        mix_u(0, u_first[:, :, 0:P], 0, P, False)
-        mix_u(0, u_first[:, :, P : 2 * P], P, 2 * P, True)
-        mix_u(0, u_first[:, :, 2 * P : M], 2 * P, M, True)
-        quantise_u(0, 0, 2 * P)
-        for piece, (lo, hi) in enumerate(U_PIECES):
-            for m in range(lo // P, hi // P):
-                cols = slice(P * m, P * (m + 1))
-                mix_u(1, u_last[piece][:, :, P * m - lo : P * (m + 1) - lo], P * m, P * (m + 1), m == 1)
-                quantise_u(1, P * m, P * (m + 1))
-                if m == 0:
-                    quantise_u(0, 2 * P, M)
-                for part in [part for part in parts if part[0] == m]:
-                    times_w4(last, part)
-                    for a in range(NC):
-                        times_u(a, part)
+        last_mix = {}
+
+        def mix_last(m, on_scalar, tag=None):
+            piece = max(m - 1, 0)
+            lo = P * m - U_PIECES[piece][0]
+            last_mix[m] = held([P, P, 4], BF16, "last_mix%d" % m, tag)
+            mix(on_scalar, last_mix[m][:], u_last[piece][:, :, lo : lo + P])
+
+        def close(m):
+            last_codes[m] = held([P, P], U32, "last_codes%d" % m)
+            quantise(last_codes[m][:], u_scale[1][:, P * m : P * (m + 1)], last_mix[m][:])
+            for part in parts:
+                if part[0] == m:
+                    times_u(1, part)
                     finish(part)
+
+        for part in parts:
+            times_w4(last, part)
+        mix_first(0, 1, True)
+        mix_first(1, 2, True)
+        mix_first(2, 4, True)
+        first_pass(0, 1)
+        mix_last(0, False)
+        mix_last(1, False)
+        close(0)
+        first_pass(1, 2)
+        close(1)
+        first_pass(2, 4)
+        mix_last(2, True)
+        close(2)
+        mix_last(3, False, "last_codes1")
+        close(3)

@@ -120,14 +120,14 @@ def tile_list_hmix_gelu_kernel(tc, xT, w4_words, w4_scales, c, u, wgt, b, offs, 
         nc.gpsimd.memset(b_rows[:], 0.0)
         nc.gpsimd.memset(warm[:], 0.0)
         make_identity(nc, ident[:])
-        nc.scalar.activation(warm[:], warm[:], GELU)
 
         nc.sync.dma_start(w_dealt[:], wgt.rearrange("r (h w) -> (r h) w", h=2)[0 : 2 * P : 17, :])
         nc.sync.dma_start(offsets[:], offs)
         for a in range(NX):
             rows = xT[KP * a : KP * (a + 1), :].rearrange("(p i) t -> p i t", i=4)
             for i in range(4):
-                nc.sync.dma_start(planes[a][i][:], rows[:, i, :])
+                queue = nc.scalar if 4 * a + i in (0, 2, 4) else nc.sync
+                queue.dma_start(planes[a][i][:], rows[:, i, :])
                 if a > 0 and i == 1:
                     load_rows(c_raw[a - 1], c, a - 1, 0, S)
                 if a == 1:
@@ -144,6 +144,7 @@ def tile_list_hmix_gelu_kernel(tc, xT, w4_words, w4_scales, c, u, wgt, b, offs, 
         for piece, (lo, hi) in enumerate(U_PIECES):
             load_rows(u_last[piece], u, 1, lo, hi)
 
+        nc.scalar.activation(warm[:], warm[:], GELU)
         nc.vector.transpose(w_turned[:], w_dealt[:])
         nc.vector.tensor_copy(
             w_spread[:].rearrange("p (c h r) -> p c h r", h=2, r=16),

@@ -1,7 +1,6 @@
 from contextlib import ExitStack
 
 import concourse.mybir as mybir
-from concourse.masks import make_identity
 
 K, L, M, T, S = 1536, 1024, 512, 1024, 512
 FLOPS = 2 * M * S * (K + L)
@@ -22,8 +21,12 @@ KP = 512
 NX, NC = K // KP, L // KP
 NM = M // P
 H = S // 2
+PLANES = 4 * NX
 
-U_PIECES = ((0, 2 * P), (2 * P, 3 * P), (3 * P, 4 * P))
+C_BEHIND = (5, 8)
+W_BEHIND = 10
+B_BEHIND = 3
+ON_SCALAR_QUEUE = (0, 2, 4)
 
 
 def tile_list_hmix_gelu_kernel(tc, xT, w4_words, w4_scales, c, u, wgt, b, offs, out):
@@ -40,31 +43,30 @@ def tile_list_hmix_gelu_kernel(tc, xT, w4_words, w4_scales, c, u, wgt, b, offs, 
         w_turned = held([P, 32], F32, "w_turned")
         w_spread = held([P, S], F32, "w_spread")
         weight = held([P, S], F32, "weight")
-        planes = [[held([P, T], F32, "plane%d_%d" % (a, i)) for i in range(4)] for a in range(NX)]
+        b_dealt = held([P, 32], F32, "b_dealt")
+        b_cols = held([P, 32], F32, "b_cols")
+        warm = held([P, 1], F32, "warm")
+        planes = [held([P, T], F32, "plane%d" % n) for n in range(PLANES)]
         picked = [held([P, 4, S], F32, "picked%d" % a) for a in range(NX)]
         c_raw = [held([P, 4, S], F32, "c_raw%d" % a) for a in range(NC)]
         u_first = held([P, 4, M], F32, "u_first")
-        u_last = [held([P, 4, hi - lo], F32, "u_last%d" % lo) for lo, hi in U_PIECES]
-        mixed = [held([P, S * (1 + min(a, 1)), 4], BF16, "mixed%d" % a) for a in range(NX)]
-        scales = [held([P, S * (1 + min(a, 1))], U8, "scales%d" % a) for a in range(NX)]
-        x_mix = [tile[:, 0:S, :] for tile in mixed]
-        c_mix = [tile[:, S : 2 * S, :] for tile in mixed[1:]]
-        u_mix = held([P, M, 4], BF16, "u_mix")
-        u_codes = held([P, M], U32, "u_codes")
-        u_scale = [held([P, M], U8, "u_scale%d" % a) for a in range(NC)]
-        last_codes = {}
+        u_last = [held([P, 4, 2 * P], F32, "u_last%d" % h) for h in range(2)]
+        x_mix = [held([P, S, 4], BF16, "x_mix%d" % a) for a in range(NX)]
+        c_mix = [held([P, S, 4], BF16, "c_mix%d" % a) for a in range(NC)]
+        first_mix = [held([P, 2 * P, 4], BF16, "first_mix%d" % h) for h in range(2)]
+        last_mix = [held([P, P, 4], BF16, "last_mix%d" % m) for m in range(NM)]
+        x_scale = [held([P, S], U8, "x_scale%d" % a) for a in range(NX)]
+        c_scale = [held([P, S], U8, "c_scale%d" % a) for a in range(NC)]
+        first_scale = [held([P, 2 * P], U8, "first_scale%d" % h) for h in range(2)]
+        last_scale = [held([P, P], U8, "last_scale%d" % m) for m in range(NM)]
+        last_codes = [held([P, P], U32, "last_codes%d" % m) for m in range(NM)]
         w_first = held([P, 2 * M], U8, "w_first")
         w_rest = held([P, NX - 1, 2 * M], U8, "w_rest")
         w_words = [w_first[:]] + [w_rest[:, a, :] for a in range(NX - 1)]
         w_scale = held([P, NX, M], U8, "w_scale")
-        b_rows = held([P, P], F32, "b_rows")
-        b_cols = held([P, NM], F32, "b_cols")
-        ident = held([P, P], F32, "ident")
-        warm = held([P, 1], F32, "warm")
         result = [held([P, S], F32, "result%d" % m) for m in range(NM)]
-        parts = [(m, 0, S) for m in range(NM - 1)] + [(NM - 1, 0, H), (NM - 1, H, S)]
+        parts = [(0, 0, H), (0, H, S), (1, 0, S), (2, 0, S), (3, 0, H), (3, H, S)]
         sums = {part: psum.tile([P, part[2] - part[1]], F32, name="sums%d_%d" % part[:2]) for part in parts}
-        b_turned = psum.tile([P, P], F32, name="b_turned")
 
         def load_rows(tile, src, a, lo, hi):
             rows = src[KP * a : KP * (a + 1), :].rearrange("(p i) w -> p i w", i=4)
@@ -81,68 +83,47 @@ def tile_list_hmix_gelu_kernel(tc, xT, w4_words, w4_scales, c, u, wgt, b, offs, 
         def quantise(words, scale, values):
             nc.vector.quantize_mx(out=words.bitcast(FP8X4), scales=scale, in_=values.rearrange("p w i -> p (w i)"))
 
-        def gather(a, i, lo, hi):
+        def gather(n, lo, hi):
             listed = offsets[:, lo // 16 : hi // 16]
-            nc.vector.tensor_tensor(picked[a][:, i, lo:hi], planes[a][i][:].indirect(listed), weight[:, lo:hi], MULT)
+            nc.vector.tensor_tensor(picked[n // 4][:, n % 4, lo:hi], planes[n][:].indirect(listed), weight[:, lo:hi], MULT)
 
-        def times_w4(a, part):
-            m, lo, hi = part
-            width = S if hi - lo == S else P
-            for at in range(lo, hi, width):
-                nc.tensor.matmul_mx(
-                    out=sums[part][:, at - lo : at - lo + width],
-                    lhsT=w_words[a][:, 2 * P * m : 2 * P * (m + 1)].bitcast(FP4X4),
-                    lhsT_scale=w_scale[:, a, P * m : P * (m + 1)],
-                    rhs=codes[a][:, at : at + width].bitcast(FP8X4),
-                    rhs_scale=scales[a][:, at : at + width],
-                    start=a == 0 and at == lo,
-                    stop=False,
-                )
-
-        def times_u(a, part):
+        def multiply(part, fixed, fixed_scale, moving, moving_scale, start=False, stop=False):
             m, lo, hi = part
             nc.tensor.matmul_mx(
                 out=sums[part][:],
-                lhsT=(last_codes[m][:] if a == NC - 1 else u_codes[:, P * m : P * (m + 1)]).bitcast(FP8X4),
-                lhsT_scale=u_scale[a][:, P * m : P * (m + 1)],
-                rhs=codes[a + 1][:, S + lo : S + hi].bitcast(FP8X4),
-                rhs_scale=scales[a + 1][:, S + lo : S + hi],
-                start=False,
-                stop=a == NC - 1,
+                lhsT=fixed,
+                lhsT_scale=fixed_scale,
+                rhs=moving[:, lo:hi].bitcast(FP8X4),
+                rhs_scale=moving_scale[:, lo:hi],
+                start=start,
+                stop=stop,
             )
 
-        def finish(part):
-            m, lo, hi = part
-            nc.scalar.activation(result[m][:, lo:hi], sums[part][:], GELU, bias=b_cols[:, m : m + 1])
-            nc.sync.dma_start(out[P * m : P * (m + 1), lo:hi], result[m][:, lo:hi])
-
-        nc.gpsimd.memset(w_scale[:].rearrange("p a n -> p (a n)").bitcast(I32), 0)
-        nc.gpsimd.memset(b_rows[:], 0.0)
         nc.gpsimd.memset(warm[:], 0.0)
-        make_identity(nc, ident[:])
+        nc.gpsimd.memset(b_dealt[:], 0.0)
+        nc.gpsimd.memset(w_scale[:].rearrange("p a n -> p (a n)").bitcast(I32), 0)
 
         nc.sync.dma_start(w_dealt[:], wgt.rearrange("r (h w) -> (r h) w", h=2)[0 : 2 * P : 17, :])
         nc.sync.dma_start(offsets[:], offs)
-        for a in range(NX):
-            rows = xT[KP * a : KP * (a + 1), :].rearrange("(p i) t -> p i t", i=4)
-            for i in range(4):
-                queue = nc.scalar if 4 * a + i in (0, 2, 4) else nc.sync
-                queue.dma_start(planes[a][i][:], rows[:, i, :])
-                if a > 0 and i == 1:
-                    load_rows(c_raw[a - 1], c, a - 1, 0, S)
-                if a == 1:
+        for n in range(PLANES):
+            rows = xT[KP * (n // 4) : KP * (n // 4 + 1), :].rearrange("(p i) t -> p i t", i=4)
+            queue = nc.scalar if n in ON_SCALAR_QUEUE else nc.sync
+            queue.dma_start(planes[n][:], rows[:, n % 4, :])
+            if n == B_BEHIND:
+                nc.sync.dma_start(b_dealt[0:P:8, :], b.rearrange("(m q w) -> q m w", q=4, w=32))
+            if n in C_BEHIND:
+                load_rows(c_raw[C_BEHIND.index(n)], c, C_BEHIND.index(n), 0, S)
+            if n == W_BEHIND:
+                for r in range(4):
                     nc.sync.dma_start(
-                        w_scale[i:P:32, :, :].bitcast(I32),
-                        w4_scales[:, i:16:4, :].rearrange("a q n -> q a n").bitcast(I32),
+                        w_scale[r:P:32, :, :].bitcast(I32),
+                        w4_scales[:, r:16:4, :].rearrange("a q n -> q a n").bitcast(I32),
                     )
-                if (a, i) == (1, 3):
-                    nc.sync.dma_start(w_first[:].bitcast(I32), w4_words[0].bitcast(I32))
-                if (a, i) == (0, 3):
-                    nc.sync.dma_start(b_rows[0:NM, :], b.rearrange("(m p) -> m p", p=P))
+                nc.sync.dma_start(w_first[:], w4_words[0])
         nc.sync.dma_start(w_rest[:], w4_words[1:NX].rearrange("a p n -> p a n"))
         load_rows(u_first, u, 0, 0, M)
-        for piece, (lo, hi) in enumerate(U_PIECES):
-            load_rows(u_last[piece], u, 1, lo, hi)
+        for h in range(2):
+            load_rows(u_last[h], u, 1, 2 * P * h, 2 * P * (h + 1))
 
         nc.scalar.activation(warm[:], warm[:], GELU)
         nc.vector.transpose(w_turned[:], w_dealt[:])
@@ -152,75 +133,85 @@ def tile_list_hmix_gelu_kernel(tc, xT, w4_words, w4_scales, c, u, wgt, b, offs, 
         )
         nc.vector.transpose(weight[:], w_spread[:])
 
-        codes = []
+        x_codes, c_codes = {}, {}
+
+        def quantise_x(a, tag=None):
+            x_codes[a] = held([P, S], U32, "x_codes%d" % a, tag)
+            quantise(x_codes[a][:], x_scale[a][:], x_mix[a][:])
+
+        def quantise_c(a, tag=None):
+            c_codes[a] = held([P, S], U32, "c_codes%d" % a, tag)
+            quantise(c_codes[a][:], c_scale[a][:], c_mix[a][:])
+
         last = NX - 1
-        for a in range(NX):
-            for i in range(4):
-                if (a, i) == (last, 3):
-                    gather(a, i, 0, H)
-                    gather(a, i, H, S)
-                else:
-                    gather(a, i, 0, S)
-                if (a, i) == (last, 1):
-                    mix(True, x_mix[a][:, :, 0:2], picked[a][:, 0:2, :])
-                if a > 0 and i == 1:
-                    mix(True, c_mix[a - 1], c_raw[a - 1][:])
-                if a > 0 and i == 1:
-                    codes.append(held([P, S * a], U32, "codes%d" % (a - 1), "plane%d_1" % a))
-                    quantise(codes[a - 1][:], scales[a - 1][:], mixed[a - 1][:])
-            if a < last:
-                mix(True, x_mix[a], picked[a][:])
+        for n in range(PLANES - 1):
+            gather(n, 0, S)
+            if n in (3, 7):
+                mix(True, x_mix[n // 4][:], picked[n // 4][:])
+            if n in C_BEHIND:
+                mix(True, c_mix[C_BEHIND.index(n)][:], c_raw[C_BEHIND.index(n)][:])
+            if n == 5:
+                quantise_x(0, "plane5")
+                nc.vector.transpose(b_cols[:], b_dealt[:])
+            if n == 8:
+                quantise_c(0, "plane7")
+                quantise_x(1)
+            if n == 9:
+                mix(True, x_mix[last][:, :, 0:2], picked[last][:, 0:2, :])
+            if n == 10:
+                quantise_c(1)
+        gather(PLANES - 1, 0, H)
+        gather(PLANES - 1, H, S)
         mix(True, x_mix[last][:, 0:H, 2:4], picked[last][:, 2:4, 0:H])
         mix(False, x_mix[last][:, H:S, 2:4], picked[last][:, 2:4, H:S])
-        nc.tensor.transpose(b_turned[:], b_rows[:], ident[:])
-        nc.scalar.copy(b_cols[:], b_turned[:, 0:NM])
-        codes.append(held([P, 2 * S], U32, "codes%d" % last, "plane%d_3" % last))
-        for cols in (slice(0, S), slice(S, 2 * S)):
-            quantise(codes[last][:, cols], scales[last][:, cols], mixed[last][:, cols, :])
+        x_codes[last] = held([P, S], U32, "x_codes%d" % last)
+        for cols in (slice(0, H), slice(H, S)):
+            quantise(x_codes[last][:, cols], x_scale[last][:, cols], x_mix[last][:, cols, :])
 
-        for a in range(last):
+        for a in range(NX):
             for part in parts:
-                times_w4(a, part)
+                m = part[0]
+                multiply(
+                    part,
+                    w_words[a][:, 2 * P * m : 2 * P * (m + 1)].bitcast(FP4X4),
+                    w_scale[:, a, P * m : P * (m + 1)],
+                    x_codes[a],
+                    x_scale[a],
+                    start=a == 0,
+                )
 
-        def mix_first(lo, hi, on_scalar):
-            mix(on_scalar, u_mix[:, P * lo : P * hi, :], u_first[:, :, P * lo : P * hi])
+        def first_codes(h, tag=None):
+            codes = held([P, 2 * P], U32, "first_codes%d" % h, tag)
+            quantise(codes[:], first_scale[h][:], first_mix[h][:])
+            return codes
 
-        def first_pass(lo, hi):
-            cols = slice(P * lo, P * hi)
-            quantise(u_codes[:, cols], u_scale[0][:, cols], u_mix[:, cols, :])
+        def first_pass(h, codes):
             for part in parts:
-                if lo <= part[0] < hi:
-                    times_u(0, part)
+                if part[0] // 2 == h:
+                    cols = slice(P * (part[0] % 2), P * (part[0] % 2 + 1))
+                    multiply(part, codes[:, cols].bitcast(FP8X4), first_scale[h][:, cols], c_codes[0], c_scale[0])
 
-        last_mix = {}
-
-        def mix_last(m, on_scalar, tag=None):
-            piece = max(m - 1, 0)
-            lo = P * m - U_PIECES[piece][0]
-            last_mix[m] = held([P, P, 4], BF16, "last_mix%d" % m, tag)
-            mix(on_scalar, last_mix[m][:], u_last[piece][:, :, lo : lo + P])
+        def mix_last(m, on_scalar):
+            mix(on_scalar, last_mix[m][:], u_last[m // 2][:, :, P * (m % 2) : P * (m % 2 + 1)])
 
         def close(m):
-            last_codes[m] = held([P, P], U32, "last_codes%d" % m)
-            quantise(last_codes[m][:], u_scale[1][:, P * m : P * (m + 1)], last_mix[m][:])
+            quantise(last_codes[m][:], last_scale[m][:], last_mix[m][:])
             for part in parts:
                 if part[0] == m:
-                    times_u(1, part)
-                    finish(part)
+                    multiply(part, last_codes[m][:].bitcast(FP8X4), last_scale[m][:], c_codes[1], c_scale[1], stop=True)
+                    lo, hi = part[1:]
+                    nc.scalar.activation(result[m][:, lo:hi], sums[part][:], GELU, bias=b_cols[:, 8 * m : 8 * m + 1])
+                    nc.sync.dma_start(out[P * m : P * (m + 1), lo:hi], result[m][:, lo:hi])
 
-        for part in parts:
-            times_w4(last, part)
-        mix_first(0, 1, True)
-        mix_first(1, 2, True)
-        mix_first(2, 4, True)
-        first_pass(0, 1)
+        for h in range(2):
+            mix(h == 0, first_mix[h][:], u_first[:, :, 2 * P * h : 2 * P * (h + 1)])
+        first_pass(0, first_codes(0))
         mix_last(0, False)
-        mix_last(1, False)
+        mix_last(1, True)
         close(0)
-        first_pass(1, 2)
         close(1)
-        first_pass(2, 4)
-        mix_last(2, True)
+        first_pass(1, first_codes(1, "last_mix0"))
+        mix_last(2, False)
+        mix_last(3, False)
         close(2)
-        mix_last(3, False, "last_codes1")
         close(3)

@@ -23,8 +23,8 @@ NM = M // P
 H = S // 2
 PLANES = 4 * NX
 
-C_BEHIND = (5, 8)
-W_BEHIND = 10
+C_BEHIND = (5, 9)
+W_BEHIND = 7
 B_BEHIND = 3
 ON_SCALAR_QUEUE = (0, 2, 4)
 
@@ -51,13 +51,16 @@ def tile_list_hmix_gelu_kernel(tc, xT, w4_words, w4_scales, c, u, wgt, b, offs, 
         c_raw = [held([P, 4, S], F32, "c_raw%d" % a) for a in range(NC)]
         u_first = held([P, 4, M], F32, "u_first")
         u_last = [held([P, 4, 2 * P], F32, "u_last%d" % h) for h in range(2)]
-        x_mix = [held([P, S, 4], BF16, "x_mix%d" % a) for a in range(NX)]
-        c_mix = [held([P, S, 4], BF16, "c_mix%d" % a) for a in range(NC)]
+        both_mix = held([P, 2 * S, 4], BF16, "both_mix")
+        both_scale = held([P, 2 * S], U8, "both_scale")
+        x_mix = [held([P, S, 4], BF16, "x_mix0")[:], both_mix[:, 0:S, :], held([P, S, 4], BF16, "x_mix2")[:]]
+        c_mix = [both_mix[:, S : 2 * S, :], held([P, S, 4], BF16, "c_mix1")[:]]
         first_mix = [held([P, 2 * P, 4], BF16, "first_mix%d" % h) for h in range(2)]
-        last_mix = [held([P, P, 4], BF16, "last_mix%d" % m) for m in range(NM)]
-        x_scale = [held([P, S], U8, "x_scale%d" % a) for a in range(NX)]
-        c_scale = [held([P, S], U8, "c_scale%d" % a) for a in range(NC)]
-        first_scale = [held([P, 2 * P], U8, "first_scale%d" % h) for h in range(2)]
+        first_codes = held([P, M], U32, "first_codes")
+        first_scale = held([P, M], U8, "first_scale")
+        last_mix = {}
+        x_scale = [held([P, S], U8, "x_scale0")[:], both_scale[:, 0:S], held([P, S], U8, "x_scale2")[:]]
+        c_scale = [both_scale[:, S : 2 * S], held([P, S], U8, "c_scale1")[:]]
         last_scale = [held([P, P], U8, "last_scale%d" % m) for m in range(NM)]
         last_codes = [held([P, P], U32, "last_codes%d" % m) for m in range(NM)]
         w_first = held([P, 2 * M], U8, "w_first")
@@ -134,39 +137,31 @@ def tile_list_hmix_gelu_kernel(tc, xT, w4_words, w4_scales, c, u, wgt, b, offs, 
         nc.vector.transpose(weight[:], w_spread[:])
 
         x_codes, c_codes = {}, {}
-
-        def quantise_x(a, tag=None):
-            x_codes[a] = held([P, S], U32, "x_codes%d" % a, tag)
-            quantise(x_codes[a][:], x_scale[a][:], x_mix[a][:])
-
-        def quantise_c(a, tag=None):
-            c_codes[a] = held([P, S], U32, "c_codes%d" % a, tag)
-            quantise(c_codes[a][:], c_scale[a][:], c_mix[a][:])
-
         last = NX - 1
         for n in range(PLANES - 1):
             gather(n, 0, S)
             if n in (3, 7):
-                mix(True, x_mix[n // 4][:], picked[n // 4][:])
-            if n in C_BEHIND:
-                mix(True, c_mix[C_BEHIND.index(n)][:], c_raw[C_BEHIND.index(n)][:])
-            if n == 5:
-                quantise_x(0, "plane5")
-                nc.vector.transpose(b_cols[:], b_dealt[:])
-            if n == 8:
-                quantise_c(0, "plane7")
-                quantise_x(1)
+                mix(True, x_mix[n // 4], picked[n // 4][:])
             if n == 9:
                 mix(True, x_mix[last][:, :, 0:2], picked[last][:, 0:2, :])
-            if n == 10:
-                quantise_c(1)
+            if n in C_BEHIND:
+                mix(True, c_mix[C_BEHIND.index(n)], c_raw[C_BEHIND.index(n)][:])
+            if n == C_BEHIND[0]:
+                x_codes[0] = held([P, S], U32, "x_codes0", "plane%d" % n)[:]
+                quantise(x_codes[0], x_scale[0], x_mix[0])
+                nc.vector.transpose(b_cols[:], b_dealt[:])
+            if n == C_BEHIND[1]:
+                both_codes = held([P, 2 * S], U32, "both_codes", "plane%d" % n)
+                quantise(both_codes[:], both_scale[:], both_mix[:])
+                x_codes[1], c_codes[0] = both_codes[:, 0:S], both_codes[:, S : 2 * S]
         gather(PLANES - 1, 0, H)
         gather(PLANES - 1, H, S)
         mix(True, x_mix[last][:, 0:H, 2:4], picked[last][:, 2:4, 0:H])
+        last_plane = held([P, 2 * S], U32, "late_codes", "plane%d" % (PLANES - 1))
+        c_codes[1], x_codes[last] = last_plane[:, 0:S], last_plane[:, S : 2 * S]
         mix(False, x_mix[last][:, H:S, 2:4], picked[last][:, 2:4, H:S])
-        x_codes[last] = held([P, S], U32, "x_codes%d" % last)
-        for cols in (slice(0, H), slice(H, S)):
-            quantise(x_codes[last][:, cols], x_scale[last][:, cols], x_mix[last][:, cols, :])
+        quantise(x_codes[last], x_scale[last], x_mix[last])
+        quantise(c_codes[1], c_scale[1], c_mix[1])
 
         for a in range(NX):
             for part in parts:
@@ -180,22 +175,27 @@ def tile_list_hmix_gelu_kernel(tc, xT, w4_words, w4_scales, c, u, wgt, b, offs, 
                     start=a == 0,
                 )
 
-        def first_codes(h, tag=None):
-            codes = held([P, 2 * P], U32, "first_codes%d" % h, tag)
-            quantise(codes[:], first_scale[h][:], first_mix[h][:])
-            return codes
+        def first_values(lo, hi):
+            half = lo // 2
+            return first_mix[half][:, P * (lo - 2 * half) : P * (hi - 2 * half), :]
 
-        def first_pass(h, codes):
+        def mix_first(lo, hi, on_scalar):
+            mix(on_scalar, first_values(lo, hi), u_first[:, :, P * lo : P * hi])
+
+        def first_pass(lo, hi):
+            cols = slice(P * lo, P * hi)
+            quantise(first_codes[:, cols], first_scale[:, cols], first_values(lo, hi))
             for part in parts:
-                if part[0] // 2 == h:
-                    cols = slice(P * (part[0] % 2), P * (part[0] % 2 + 1))
-                    multiply(part, codes[:, cols].bitcast(FP8X4), first_scale[h][:, cols], c_codes[0], c_scale[0])
+                if lo <= part[0] < hi:
+                    cols = slice(P * part[0], P * (part[0] + 1))
+                    multiply(part, first_codes[:, cols].bitcast(FP8X4), first_scale[:, cols], c_codes[0], c_scale[0])
 
-        def mix_last(m, on_scalar):
-            mix(on_scalar, last_mix[m][:], u_last[m // 2][:, :, P * (m % 2) : P * (m % 2 + 1)])
+        def mix_last(m, on_scalar, values):
+            last_mix[m] = values
+            mix(on_scalar, last_mix[m], u_last[m // 2][:, :, P * (m % 2) : P * (m % 2 + 1)])
 
         def close(m):
-            quantise(last_codes[m][:], last_scale[m][:], last_mix[m][:])
+            quantise(last_codes[m][:], last_scale[m][:], last_mix[m])
             for part in parts:
                 if part[0] == m:
                     multiply(part, last_codes[m][:].bitcast(FP8X4), last_scale[m][:], c_codes[1], c_scale[1], stop=True)
@@ -203,15 +203,17 @@ def tile_list_hmix_gelu_kernel(tc, xT, w4_words, w4_scales, c, u, wgt, b, offs, 
                     nc.scalar.activation(result[m][:, lo:hi], sums[part][:], GELU, bias=b_cols[:, 8 * m : 8 * m + 1])
                     nc.sync.dma_start(out[P * m : P * (m + 1), lo:hi], result[m][:, lo:hi])
 
-        for h in range(2):
-            mix(h == 0, first_mix[h][:], u_first[:, :, 2 * P * h : 2 * P * (h + 1)])
-        first_pass(0, first_codes(0))
-        mix_last(0, False)
-        mix_last(1, True)
+        for lo, hi in ((0, 1), (1, 2), (2, 4)):
+            mix_first(lo, hi, True)
+        first_pass(0, 1)
+        for m in range(2):
+            mix_last(m, False, held([P, P, 4], BF16, "last_mix%d" % m)[:])
         close(0)
+        first_pass(1, 2)
         close(1)
-        first_pass(1, first_codes(1, "last_mix0"))
-        mix_last(2, False)
-        mix_last(3, False)
+        first_pass(2, 4)
+        late_mix = held([P, 2 * P, 4], BF16, "late_mix", "first_mix1")
+        for m in range(2, NM):
+            mix_last(m, False, late_mix[:, P * (m - 2) : P * (m - 1), :])
         close(2)
         close(3)

@@ -27,6 +27,7 @@ C_BEHIND = (5, 9)
 W_BEHIND = 7
 B_BEHIND = 3
 ON_SCALAR_QUEUE = (0, 2, 4)
+U_PIECES = ((0, 2 * P), (2 * P, 3 * P), (3 * P, 4 * P))
 
 
 def tile_list_hmix_gelu_kernel(tc, xT, w4_words, w4_scales, c, u, wgt, b, offs, out):
@@ -50,7 +51,7 @@ def tile_list_hmix_gelu_kernel(tc, xT, w4_words, w4_scales, c, u, wgt, b, offs, 
         picked = [held([P, 4, S], F32, "picked%d" % a) for a in range(NX)]
         c_raw = [held([P, 4, S], F32, "c_raw%d" % a) for a in range(NC)]
         u_first = held([P, 4, M], F32, "u_first")
-        u_last = [held([P, 4, 2 * P], F32, "u_last%d" % h) for h in range(2)]
+        u_last = [held([P, 4, hi - lo], F32, "u_last%d" % lo) for lo, hi in U_PIECES]
         both_mix = held([P, 2 * S, 4], BF16, "both_mix")
         both_scale = held([P, 2 * S], U8, "both_scale")
         x_mix = [held([P, S, 4], BF16, "x_mix0")[:], both_mix[:, 0:S, :], held([P, S, 4], BF16, "x_mix2")[:]]
@@ -68,7 +69,7 @@ def tile_list_hmix_gelu_kernel(tc, xT, w4_words, w4_scales, c, u, wgt, b, offs, 
         w_words = [w_first[:]] + [w_rest[:, a, :] for a in range(NX - 1)]
         w_scale = held([P, NX, M], U8, "w_scale")
         result = [held([P, S], F32, "result%d" % m) for m in range(NM)]
-        parts = [(0, 0, H), (0, H, S), (1, 0, S), (2, 0, S), (3, 0, H), (3, H, S)]
+        parts = [(0, 0, S), (1, 0, S), (2, 0, S), (3, 0, H), (3, H, S)]
         sums = {part: psum.tile([P, part[2] - part[1]], F32, name="sums%d_%d" % part[:2]) for part in parts}
 
         def load_rows(tile, src, a, lo, hi):
@@ -125,8 +126,8 @@ def tile_list_hmix_gelu_kernel(tc, xT, w4_words, w4_scales, c, u, wgt, b, offs, 
                 nc.sync.dma_start(w_first[:], w4_words[0])
         nc.sync.dma_start(w_rest[:], w4_words[1:NX].rearrange("a p n -> p a n"))
         load_rows(u_first, u, 0, 0, M)
-        for h in range(2):
-            load_rows(u_last[h], u, 1, 2 * P * h, 2 * P * (h + 1))
+        for piece, (lo, hi) in enumerate(U_PIECES):
+            load_rows(u_last[piece], u, 1, lo, hi)
 
         nc.scalar.activation(warm[:], warm[:], GELU)
         nc.vector.transpose(w_turned[:], w_dealt[:])
@@ -156,12 +157,12 @@ def tile_list_hmix_gelu_kernel(tc, xT, w4_words, w4_scales, c, u, wgt, b, offs, 
                 x_codes[1], c_codes[0] = both_codes[:, 0:S], both_codes[:, S : 2 * S]
         gather(PLANES - 1, 0, H)
         gather(PLANES - 1, H, S)
-        mix(True, x_mix[last][:, 0:H, 2:4], picked[last][:, 2:4, 0:H])
-        last_plane = held([P, 2 * S], U32, "late_codes", "plane%d" % (PLANES - 1))
-        c_codes[1], x_codes[last] = last_plane[:, 0:S], last_plane[:, S : 2 * S]
-        mix(False, x_mix[last][:, H:S, 2:4], picked[last][:, 2:4, H:S])
-        quantise(x_codes[last], x_scale[last], x_mix[last])
+        mix(False, x_mix[last][:, 0:H, 2:4], picked[last][:, 2:4, 0:H])
+        mix(True, x_mix[last][:, H:S, 2:4], picked[last][:, 2:4, H:S])
+        late_codes = held([P, 2 * S], U32, "late_codes", "plane%d" % (PLANES - 1))
+        c_codes[1], x_codes[last] = late_codes[:, 0:S], late_codes[:, S : 2 * S]
         quantise(c_codes[1], c_scale[1], c_mix[1])
+        quantise(x_codes[last], x_scale[last], x_mix[last])
 
         for a in range(NX):
             for part in parts:
@@ -192,7 +193,9 @@ def tile_list_hmix_gelu_kernel(tc, xT, w4_words, w4_scales, c, u, wgt, b, offs, 
 
         def mix_last(m, on_scalar, values):
             last_mix[m] = values
-            mix(on_scalar, last_mix[m], u_last[m // 2][:, :, P * (m % 2) : P * (m % 2 + 1)])
+            piece = max(m - 1, 0)
+            lo = P * m - U_PIECES[piece][0]
+            mix(on_scalar, last_mix[m], u_last[piece][:, :, lo : lo + P])
 
         def close(m):
             quantise(last_codes[m][:], last_scale[m][:], last_mix[m])
@@ -203,8 +206,8 @@ def tile_list_hmix_gelu_kernel(tc, xT, w4_words, w4_scales, c, u, wgt, b, offs, 
                     nc.scalar.activation(result[m][:, lo:hi], sums[part][:], GELU, bias=b_cols[:, 8 * m : 8 * m + 1])
                     nc.sync.dma_start(out[P * m : P * (m + 1), lo:hi], result[m][:, lo:hi])
 
-        for lo, hi in ((0, 1), (1, 2), (2, 4)):
-            mix_first(lo, hi, True)
+        for m in range(NM):
+            mix_first(m, m + 1, m < NM - 1)
         first_pass(0, 1)
         for m in range(2):
             mix_last(m, False, held([P, P, 4], BF16, "last_mix%d" % m)[:])
@@ -212,8 +215,7 @@ def tile_list_hmix_gelu_kernel(tc, xT, w4_words, w4_scales, c, u, wgt, b, offs, 
         first_pass(1, 2)
         close(1)
         first_pass(2, 4)
-        late_mix = held([P, 2 * P, 4], BF16, "late_mix", "first_mix1")
-        for m in range(2, NM):
-            mix_last(m, False, late_mix[:, P * (m - 2) : P * (m - 1), :])
+        mix_last(2, True, held([P, P, 4], BF16, "last_mix2")[:])
         close(2)
+        mix_last(3, False, held([P, P, 4], BF16, "last_mix3", "u_last%d" % U_PIECES[1][0])[:])
         close(3)

@@ -64,9 +64,8 @@ def tile_list_hmix_gelu_kernel(tc, xT, w4_words, w4_scales, c, u, wgt, b, offs, 
         c_scale = [both_scale[:, S : 2 * S], held([P, S], U8, "c_scale1")[:]]
         last_scale = [held([P, P], U8, "last_scale%d" % m) for m in range(NM)]
         last_codes = [held([P, P], U32, "last_codes%d" % m) for m in range(NM)]
-        w_first = held([P, 2 * M], U8, "w_first")
-        w_rest = held([P, NX - 1, 2 * M], U8, "w_rest")
-        w_words = [w_first[:]] + [w_rest[:, a, :] for a in range(NX - 1)]
+        w_main = held([P, NX, 2 * P * (NM - 1)], U8, "w_main")
+        w_tail = held([P, NX, 2 * P], U8, "w_tail")
         w_scale = held([P, NX, M], U8, "w_scale")
         result = [held([P, S], F32, "result%d" % m) for m in range(NM)]
         parts = [(0, 0, S), (1, 0, S), (2, 0, S), (3, 0, H), (3, H, S)]
@@ -123,11 +122,12 @@ def tile_list_hmix_gelu_kernel(tc, xT, w4_words, w4_scales, c, u, wgt, b, offs, 
                         w_scale[r:P:32, :, :].bitcast(I32),
                         w4_scales[:, r:16:4, :].rearrange("a q n -> q a n").bitcast(I32),
                     )
-                nc.sync.dma_start(w_first[:], w4_words[0])
-        nc.sync.dma_start(w_rest[:], w4_words[1:NX].rearrange("a p n -> p a n"))
+        words = w4_words.rearrange("a p n -> p a n")
+        nc.sync.dma_start(w_main[:], words[:, :, 0 : 2 * P * (NM - 1)])
         load_rows(u_first, u, 0, 0, M)
         for piece, (lo, hi) in enumerate(U_PIECES):
             load_rows(u_last[piece], u, 1, lo, hi)
+        nc.sync.dma_start(w_tail[:], words[:, :, 2 * P * (NM - 1) : 2 * M])
 
         nc.scalar.activation(warm[:], warm[:], GELU)
         nc.vector.transpose(w_turned[:], w_dealt[:])
@@ -164,17 +164,16 @@ def tile_list_hmix_gelu_kernel(tc, xT, w4_words, w4_scales, c, u, wgt, b, offs, 
         quantise(c_codes[1], c_scale[1], c_mix[1])
         quantise(x_codes[last], x_scale[last], x_mix[last])
 
+        def times_w4(a, part):
+            m = part[0]
+            fixed = w_tail[:, a, :] if m == NM - 1 else w_main[:, a, 2 * P * m : 2 * P * (m + 1)]
+            start = a == 0 and m < NM - 1
+            multiply(part, fixed.bitcast(FP4X4), w_scale[:, a, P * m : P * (m + 1)], x_codes[a], x_scale[a], start=start)
+
         for a in range(NX):
             for part in parts:
-                m = part[0]
-                multiply(
-                    part,
-                    w_words[a][:, 2 * P * m : 2 * P * (m + 1)].bitcast(FP4X4),
-                    w_scale[:, a, P * m : P * (m + 1)],
-                    x_codes[a],
-                    x_scale[a],
-                    start=a == 0,
-                )
+                if part[0] < NM - 1:
+                    times_w4(a, part)
 
         def first_values(lo, hi):
             half = lo // 2
@@ -189,7 +188,7 @@ def tile_list_hmix_gelu_kernel(tc, xT, w4_words, w4_scales, c, u, wgt, b, offs, 
             for part in parts:
                 if lo <= part[0] < hi:
                     cols = slice(P * part[0], P * (part[0] + 1))
-                    multiply(part, first_codes[:, cols].bitcast(FP8X4), first_scale[:, cols], c_codes[0], c_scale[0])
+                    multiply(part, first_codes[:, cols].bitcast(FP8X4), first_scale[:, cols], c_codes[0], c_scale[0], start=part[0] == NM - 1)
 
         def mix_last(m, on_scalar, values):
             last_mix[m] = values
@@ -201,6 +200,9 @@ def tile_list_hmix_gelu_kernel(tc, xT, w4_words, w4_scales, c, u, wgt, b, offs, 
             quantise(last_codes[m][:], last_scale[m][:], last_mix[m])
             for part in parts:
                 if part[0] == m:
+                    if m == NM - 1:
+                        for a in range(NX):
+                            times_w4(a, part)
                     multiply(part, last_codes[m][:].bitcast(FP8X4), last_scale[m][:], c_codes[1], c_scale[1], stop=True)
                     lo, hi = part[1:]
                     nc.scalar.activation(result[m][:, lo:hi], sums[part][:], GELU, bias=b_cols[:, 8 * m : 8 * m + 1])

@@ -23,11 +23,11 @@ NM = M // P
 H = S // 2
 PLANES = 4 * NX
 
-C_BEHIND = (5, 9)
-W_BEHIND = 7
 B_BEHIND = 3
+SCALES_BEHIND = 7
+C_BEHIND = 9
+C_SPLIT = 192
 ON_SCALAR_QUEUE = (0, 2, 4)
-U_PIECES = ((0, 2 * P), (2 * P, 3 * P), (3 * P, 4 * P))
 
 
 def tile_list_hmix_gelu_kernel(tc, xT, w4_words, w4_scales, c, u, wgt, b, offs, out):
@@ -51,21 +51,18 @@ def tile_list_hmix_gelu_kernel(tc, xT, w4_words, w4_scales, c, u, wgt, b, offs, 
         picked = [held([P, 4, S], F32, "picked%d" % a) for a in range(NX)]
         c_raw = [held([P, 4, S], F32, "c_raw%d" % a) for a in range(NC)]
         u_first = held([P, 4, M], F32, "u_first")
-        u_last = [held([P, 4, hi - lo], F32, "u_last%d" % lo) for lo, hi in U_PIECES]
-        both_mix = held([P, 2 * S, 4], BF16, "both_mix")
-        both_scale = held([P, 2 * S], U8, "both_scale")
-        x_mix = [held([P, S, 4], BF16, "x_mix0")[:], both_mix[:, 0:S, :], held([P, S, 4], BF16, "x_mix2")[:]]
-        c_mix = [both_mix[:, S : 2 * S, :], held([P, S, 4], BF16, "c_mix1")[:]]
-        first_mix = [held([P, 2 * P, 4], BF16, "first_mix%d" % h) for h in range(2)]
-        first_codes = held([P, M], U32, "first_codes")
-        first_scale = held([P, M], U8, "first_scale")
-        last_mix = {}
-        x_scale = [held([P, S], U8, "x_scale0")[:], both_scale[:, 0:S], held([P, S], U8, "x_scale2")[:]]
-        c_scale = [both_scale[:, S : 2 * S], held([P, S], U8, "c_scale1")[:]]
-        last_scale = [held([P, P], U8, "last_scale%d" % m) for m in range(NM)]
-        last_codes = [held([P, P], U32, "last_codes%d" % m) for m in range(NM)]
-        w_main = held([P, NX, 2 * P * (NM - 1)], U8, "w_main")
-        w_tail = held([P, NX, 2 * P], U8, "w_tail")
+        u_last = [held([P, 4, P], F32, "u_last%d" % m) for m in range(NM)]
+        early_mix = held([P, 2 * S, 4], BF16, "early_mix")
+        late_mix = [held([P, H, 4], BF16, "late_mix%d" % h) for h in range(2)]
+        c_mix = [held([P, S, 4], BF16, "c_mix%d" % a) for a in range(NC)]
+        u_mix = [[held([P, P, 4], BF16, "u_mix%d_%d" % (a, m)) for m in range(NM)] for a in range(NC)]
+        x_scale = held([P, NX * S], U8, "x_scale")
+        late_codes = held([P, S], U32, "late_codes")
+        c_codes = {1: held([P, S], U32, "c_codes1")}
+        c_scale = [held([P, S], U8, "c_scale%d" % a) for a in range(NC)]
+        u_codes = [held([P, M], U32, "u_codes%d" % a) for a in range(NC)]
+        u_scale = [held([P, M], U8, "u_scale%d" % a) for a in range(NC)]
+        w_words = held([P, NX, 2 * M], U8, "w_words")
         w_scale = held([P, NX, M], U8, "w_scale")
         result = [held([P, S], F32, "result%d" % m) for m in range(NM)]
         parts = [(0, 0, S), (1, 0, S), (2, 0, S), (3, 0, H), (3, H, S)]
@@ -85,10 +82,6 @@ def tile_list_hmix_gelu_kernel(tc, xT, w4_words, w4_scales, c, u, wgt, b, offs, 
 
         def quantise(words, scale, values):
             nc.vector.quantize_mx(out=words.bitcast(FP8X4), scales=scale, in_=values.rearrange("p w i -> p (w i)"))
-
-        def gather(n, lo, hi):
-            listed = offsets[:, lo // 16 : hi // 16]
-            nc.vector.tensor_tensor(picked[n // 4][:, n % 4, lo:hi], planes[n][:].indirect(listed), weight[:, lo:hi], MULT)
 
         def multiply(part, fixed, fixed_scale, moving, moving_scale, start=False, stop=False):
             m, lo, hi = part
@@ -114,20 +107,19 @@ def tile_list_hmix_gelu_kernel(tc, xT, w4_words, w4_scales, c, u, wgt, b, offs, 
             queue.dma_start(planes[n][:], rows[:, n % 4, :])
             if n == B_BEHIND:
                 nc.sync.dma_start(b_dealt[0:P:8, :], b.rearrange("(m q w) -> q m w", q=4, w=32))
-            if n in C_BEHIND:
-                load_rows(c_raw[C_BEHIND.index(n)], c, C_BEHIND.index(n), 0, S)
-            if n == W_BEHIND:
+            if n == C_BEHIND:
+                load_rows(c_raw[0], c, 0, 0, S)
+            if n == SCALES_BEHIND:
                 for r in range(4):
                     nc.sync.dma_start(
                         w_scale[r:P:32, :, :].bitcast(I32),
                         w4_scales[:, r:16:4, :].rearrange("a q n -> q a n").bitcast(I32),
                     )
-        words = w4_words.rearrange("a p n -> p a n")
-        nc.sync.dma_start(w_main[:], words[:, :, 0 : 2 * P * (NM - 1)])
+        nc.sync.dma_start(w_words[:], w4_words.rearrange("a p n -> p a n"))
+        load_rows(c_raw[1], c, 1, 0, S)
         load_rows(u_first, u, 0, 0, M)
-        for piece, (lo, hi) in enumerate(U_PIECES):
-            load_rows(u_last[piece], u, 1, lo, hi)
-        nc.sync.dma_start(w_tail[:], words[:, :, 2 * P * (NM - 1) : 2 * M])
+        for m in range(NM):
+            load_rows(u_last[m], u, 1, P * m, P * (m + 1))
 
         nc.scalar.activation(warm[:], warm[:], GELU)
         nc.vector.transpose(w_turned[:], w_dealt[:])
@@ -137,87 +129,49 @@ def tile_list_hmix_gelu_kernel(tc, xT, w4_words, w4_scales, c, u, wgt, b, offs, 
         )
         nc.vector.transpose(weight[:], w_spread[:])
 
-        x_codes, c_codes = {}, {}
-        last = NX - 1
-        for n in range(PLANES - 1):
-            gather(n, 0, S)
+        for n in range(PLANES):
+            nc.vector.tensor_tensor(picked[n // 4][:, n % 4, :], planes[n][:].indirect(offsets[:]), weight[:], MULT)
             if n in (3, 7):
-                mix(True, x_mix[n // 4], picked[n // 4][:])
-            if n == 9:
-                mix(True, x_mix[last][:, :, 0:2], picked[last][:, 0:2, :])
-            if n in C_BEHIND:
-                mix(True, c_mix[C_BEHIND.index(n)], c_raw[C_BEHIND.index(n)][:])
-            if n == C_BEHIND[0]:
-                x_codes[0] = held([P, S], U32, "x_codes0", "plane%d" % n)[:]
-                quantise(x_codes[0], x_scale[0], x_mix[0])
-                nc.vector.transpose(b_cols[:], b_dealt[:])
-            if n == C_BEHIND[1]:
-                both_codes = held([P, 2 * S], U32, "both_codes", "plane%d" % n)
-                quantise(both_codes[:], both_scale[:], both_mix[:])
-                x_codes[1], c_codes[0] = both_codes[:, 0:S], both_codes[:, S : 2 * S]
-        gather(PLANES - 1, 0, H)
-        gather(PLANES - 1, H, S)
-        mix(False, x_mix[last][:, 0:H, 2:4], picked[last][:, 2:4, 0:H])
-        mix(True, x_mix[last][:, H:S, 2:4], picked[last][:, 2:4, H:S])
-        late_codes = held([P, 2 * S], U32, "late_codes", "plane%d" % (PLANES - 1))
-        c_codes[1], x_codes[last] = late_codes[:, 0:S], late_codes[:, S : 2 * S]
-        quantise(c_codes[1], c_scale[1], c_mix[1])
-        quantise(x_codes[last], x_scale[last], x_mix[last])
+                mix(True, early_mix[:, S * (n // 4) : S * (n // 4 + 1), :], picked[n // 4][:])
+            if n == C_BEHIND:
+                early_codes = held([P, 2 * S], U32, "early_codes", "plane%d" % n)
+                quantise(early_codes[:], x_scale[:, 0 : 2 * S], early_mix[:])
+                mix(True, c_mix[0][:], c_raw[0][:])
+        for h in range(2):
+            mix(h == 1, late_mix[h][:], picked[NX - 1][:, :, H * h : H * (h + 1)])
+        c_codes[0] = held([P, S], U32, "c_codes0", "plane%d" % (PLANES - 1))
+        quantise(c_codes[0][:], c_scale[0][:], c_mix[0][:])
+        for h in range(2):
+            quantise(late_codes[:, H * h : H * (h + 1)], x_scale[:, 2 * S + H * h : 2 * S + H * (h + 1)], late_mix[h][:])
+        nc.vector.transpose(b_cols[:], b_dealt[:])
+        x_codes = [early_codes[:, 0:S], early_codes[:, S : 2 * S], late_codes[:]]
 
-        def times_w4(a, part):
-            m = part[0]
-            fixed = w_tail[:, a, :] if m == NM - 1 else w_main[:, a, 2 * P * m : 2 * P * (m + 1)]
-            start = a == 0 and m < NM - 1
-            multiply(part, fixed.bitcast(FP4X4), w_scale[:, a, P * m : P * (m + 1)], x_codes[a], x_scale[a], start=start)
+        mix(False, c_mix[1][:, 0:C_SPLIT, :], c_raw[1][:, :, 0:C_SPLIT])
+        mix(True, c_mix[1][:, C_SPLIT:S, :], c_raw[1][:, :, C_SPLIT:S])
+        quantise(c_codes[1][:], c_scale[1][:], c_mix[1][:])
 
         for a in range(NX):
             for part in parts:
-                if part[0] < NM - 1:
-                    times_w4(a, part)
+                m = part[0]
+                fixed = w_words[:, a, 2 * P * m : 2 * P * (m + 1)].bitcast(FP4X4)
+                multiply(part, fixed, w_scale[:, a, P * m : P * (m + 1)], x_codes[a], x_scale[:, S * a : S * (a + 1)], start=a == 0)
 
-        def first_values(lo, hi):
-            half = lo // 2
-            return first_mix[half][:, P * (lo - 2 * half) : P * (hi - 2 * half), :]
-
-        def mix_first(lo, hi, on_scalar):
-            mix(on_scalar, first_values(lo, hi), u_first[:, :, P * lo : P * hi])
-
-        def first_pass(lo, hi):
-            cols = slice(P * lo, P * hi)
-            quantise(first_codes[:, cols], first_scale[:, cols], first_values(lo, hi))
+        def u_pass(a, m):
+            cols = slice(P * m, P * (m + 1))
+            quantise(u_codes[a][:, cols], u_scale[a][:, cols], u_mix[a][m][:])
             for part in parts:
-                if lo <= part[0] < hi:
-                    cols = slice(P * part[0], P * (part[0] + 1))
-                    multiply(part, first_codes[:, cols].bitcast(FP8X4), first_scale[:, cols], c_codes[0], c_scale[0], start=part[0] == NM - 1)
-
-        def mix_last(m, on_scalar, values):
-            last_mix[m] = values
-            piece = max(m - 1, 0)
-            lo = P * m - U_PIECES[piece][0]
-            mix(on_scalar, last_mix[m], u_last[piece][:, :, lo : lo + P])
-
-        def close(m):
-            quantise(last_codes[m][:], last_scale[m][:], last_mix[m])
-            for part in parts:
+                left, right = part[1:]
                 if part[0] == m:
-                    if m == NM - 1:
-                        for a in range(NX):
-                            times_w4(a, part)
-                    multiply(part, last_codes[m][:].bitcast(FP8X4), last_scale[m][:], c_codes[1], c_scale[1], stop=True)
-                    lo, hi = part[1:]
-                    nc.scalar.activation(result[m][:, lo:hi], sums[part][:], GELU, bias=b_cols[:, 8 * m : 8 * m + 1])
-                    nc.sync.dma_start(out[P * m : P * (m + 1), lo:hi], result[m][:, lo:hi])
+                    multiply(part, u_codes[a][:, cols].bitcast(FP8X4), u_scale[a][:, cols], c_codes[a][:], c_scale[a][:], stop=a == NC - 1)
+                    if a == NC - 1:
+                        nc.scalar.activation(result[m][:, left:right], sums[part][:], GELU, bias=b_cols[:, 8 * m : 8 * m + 1])
+                        nc.sync.dma_start(out[P * m : P * (m + 1), left:right], result[m][:, left:right])
 
         for m in range(NM):
-            mix_first(m, m + 1, m < NM - 1)
-        first_pass(0, 1)
-        for m in range(2):
-            mix_last(m, False, held([P, P, 4], BF16, "last_mix%d" % m)[:])
-        close(0)
-        first_pass(1, 2)
-        close(1)
-        first_pass(2, 4)
-        mix_last(2, True, held([P, P, 4], BF16, "last_mix2")[:])
-        close(2)
-        mix_last(3, False, held([P, P, 4], BF16, "last_mix3", "u_last%d" % U_PIECES[1][0])[:])
-        close(3)
+            mix(m > 0, u_mix[0][m][:], u_first[:, :, P * m : P * (m + 1)])
+        u_pass(0, 0)
+        for m in range(NM):
+            mix(False, u_mix[1][m][:], u_last[m][:])
+            if m + 1 < NM:
+                u_pass(0, m + 1)
+            u_pass(1, m)

@@ -23,11 +23,11 @@ NM = M // P
 H = S // 2
 PLANES = 4 * NX
 
-B_BEHIND = 3
 SCALES_BEHIND = 7
-C_BEHIND = 9
-C_SPLIT = 192
-ON_SCALAR_QUEUE = (0, 2, 4)
+C_BEHIND = (6, 10)
+W_BEHIND = 10
+PAIRED = 2
+ON_SCALAR_QUEUE = (0,)
 
 
 def tile_list_hmix_gelu_kernel(tc, xT, w4_words, w4_scales, c, u, wgt, b, offs, out):
@@ -47,22 +47,23 @@ def tile_list_hmix_gelu_kernel(tc, xT, w4_words, w4_scales, c, u, wgt, b, offs, 
         b_dealt = held([P, 32], F32, "b_dealt")
         b_cols = held([P, 32], F32, "b_cols")
         warm = held([P, 1], F32, "warm")
-        planes = [held([P, T], F32, "plane%d" % n) for n in range(PLANES)]
+        planes = [held([P, 2 * T if n == PAIRED else T], F32, "plane%d" % n) for n in range(PLANES)]
         picked = [held([P, 4, S], F32, "picked%d" % a) for a in range(NX)]
         c_raw = [held([P, 4, S], F32, "c_raw%d" % a) for a in range(NC)]
         u_first = held([P, 4, M], F32, "u_first")
         u_last = [held([P, 4, P], F32, "u_last%d" % m) for m in range(NM)]
-        early_mix = held([P, 2 * S, 4], BF16, "early_mix")
+        both_mix = held([P, 2 * S, 4], BF16, "both_mix")
+        both_scale = held([P, 2 * S], U8, "both_scale")
+        x_mix = [held([P, S, 4], BF16, "x_mix0")[:], both_mix[:, 0:S, :]]
         late_mix = [held([P, H, 4], BF16, "late_mix%d" % h) for h in range(2)]
-        c_mix = [held([P, S, 4], BF16, "c_mix%d" % a) for a in range(NC)]
+        c_mix = [both_mix[:, S : 2 * S, :], held([P, S, 4], BF16, "c_mix1")[:]]
         u_mix = [[held([P, P, 4], BF16, "u_mix%d_%d" % (a, m)) for m in range(NM)] for a in range(NC)]
-        x_scale = held([P, NX * S], U8, "x_scale")
-        late_codes = held([P, S], U32, "late_codes")
-        c_codes = {1: held([P, S], U32, "c_codes1")}
-        c_scale = [held([P, S], U8, "c_scale%d" % a) for a in range(NC)]
+        x_scale = [held([P, S], U8, "x_scale0")[:], both_scale[:, 0:S], held([P, S], U8, "x_scale2")[:]]
+        c_scale = [both_scale[:, S : 2 * S], held([P, S], U8, "c_scale1")[:]]
         u_codes = [held([P, M], U32, "u_codes%d" % a) for a in range(NC)]
         u_scale = [held([P, M], U8, "u_scale%d" % a) for a in range(NC)]
-        w_words = held([P, NX, 2 * M], U8, "w_words")
+        w_first = held([P, 1, 2 * M], U8, "w_first")
+        w_rest = held([P, NX - 1, 2 * M], U8, "w_rest")
         w_scale = held([P, NX, M], U8, "w_scale")
         result = [held([P, S], F32, "result%d" % m) for m in range(NM)]
         parts = [(0, 0, S), (1, 0, S), (2, 0, S), (3, 0, H), (3, H, S)]
@@ -83,10 +84,9 @@ def tile_list_hmix_gelu_kernel(tc, xT, w4_words, w4_scales, c, u, wgt, b, offs, 
         def quantise(words, scale, values):
             nc.vector.quantize_mx(out=words.bitcast(FP8X4), scales=scale, in_=values.rearrange("p w i -> p (w i)"))
 
-        def multiply(part, fixed, fixed_scale, moving, moving_scale, start=False, stop=False):
-            m, lo, hi = part
+        def multiply(part, lo, hi, fixed, fixed_scale, moving, moving_scale, start=False, stop=False):
             nc.tensor.matmul_mx(
-                out=sums[part][:],
+                out=sums[part][:, lo - part[1] : hi - part[1]],
                 lhsT=fixed,
                 lhsT_scale=fixed_scale,
                 rhs=moving[:, lo:hi].bitcast(FP8X4),
@@ -95,66 +95,93 @@ def tile_list_hmix_gelu_kernel(tc, xT, w4_words, w4_scales, c, u, wgt, b, offs, 
                 stop=stop,
             )
 
-        nc.gpsimd.memset(warm[:], 0.0)
         nc.gpsimd.memset(b_dealt[:], 0.0)
+        nc.gpsimd.memset(warm[:], 0.0)
         nc.gpsimd.memset(w_scale[:].rearrange("p a n -> p (a n)").bitcast(I32), 0)
 
         nc.sync.dma_start(w_dealt[:], wgt.rearrange("r (h w) -> (r h) w", h=2)[0 : 2 * P : 17, :])
+        nc.sync.dma_start(b_dealt[0:P:8, :], b.rearrange("(m q w) -> q m w", q=4, w=32))
         nc.sync.dma_start(offsets[:], offs)
+        words = w4_words.rearrange("a p n -> p a n")
         for n in range(PLANES):
             rows = xT[KP * (n // 4) : KP * (n // 4 + 1), :].rearrange("(p i) t -> p i t", i=4)
             queue = nc.scalar if n in ON_SCALAR_QUEUE else nc.sync
-            queue.dma_start(planes[n][:], rows[:, n % 4, :])
-            if n == B_BEHIND:
-                nc.sync.dma_start(b_dealt[0:P:8, :], b.rearrange("(m q w) -> q m w", q=4, w=32))
-            if n == C_BEHIND:
-                load_rows(c_raw[0], c, 0, 0, S)
+            if n == PAIRED:
+                queue.dma_start(planes[n][:], rows[:, n % 4 : n % 4 + 2, :].rearrange("p i t -> p (i t)"))
+            elif n != PAIRED + 1:
+                queue.dma_start(planes[n][:], rows[:, n % 4, :])
+            if n in C_BEHIND:
+                load_rows(c_raw[C_BEHIND.index(n)], c, C_BEHIND.index(n), 0, S)
+            if n == W_BEHIND:
+                nc.sync.dma_start(w_first[:], words[:, 0:1, :])
             if n == SCALES_BEHIND:
                 for r in range(4):
                     nc.sync.dma_start(
                         w_scale[r:P:32, :, :].bitcast(I32),
                         w4_scales[:, r:16:4, :].rearrange("a q n -> q a n").bitcast(I32),
                     )
-        nc.sync.dma_start(w_words[:], w4_words.rearrange("a p n -> p a n"))
-        load_rows(c_raw[1], c, 1, 0, S)
+        nc.sync.dma_start(w_rest[:], words[:, 1:NX, :])
         load_rows(u_first, u, 0, 0, M)
         for m in range(NM):
             load_rows(u_last[m], u, 1, P * m, P * (m + 1))
 
         nc.scalar.activation(warm[:], warm[:], GELU)
+        nc.scalar.copy(planes[PAIRED + 1][:], planes[PAIRED][:, T : 2 * T])
         nc.vector.transpose(w_turned[:], w_dealt[:])
-        nc.vector.tensor_copy(
-            w_spread[:].rearrange("p (c h r) -> p c h r", h=2, r=16),
-            w_turned[:].rearrange("p (h c) -> p c h", h=2).unsqueeze(3).to_broadcast([P, 16, 2, 16]),
-        )
-        nc.vector.transpose(weight[:], w_spread[:])
-
-        for n in range(PLANES):
-            nc.vector.tensor_tensor(picked[n // 4][:, n % 4, :], planes[n][:].indirect(offsets[:]), weight[:], MULT)
-            if n in (3, 7):
-                mix(True, early_mix[:, S * (n // 4) : S * (n // 4 + 1), :], picked[n // 4][:])
-            if n == C_BEHIND:
-                early_codes = held([P, 2 * S], U32, "early_codes", "plane%d" % n)
-                quantise(early_codes[:], x_scale[:, 0 : 2 * S], early_mix[:])
-                mix(True, c_mix[0][:], c_raw[0][:])
-        for h in range(2):
-            mix(h == 1, late_mix[h][:], picked[NX - 1][:, :, H * h : H * (h + 1)])
-        c_codes[0] = held([P, S], U32, "c_codes0", "plane%d" % (PLANES - 1))
-        quantise(c_codes[0][:], c_scale[0][:], c_mix[0][:])
-        for h in range(2):
-            quantise(late_codes[:, H * h : H * (h + 1)], x_scale[:, 2 * S + H * h : 2 * S + H * (h + 1)], late_mix[h][:])
         nc.vector.transpose(b_cols[:], b_dealt[:])
-        x_codes = [early_codes[:, 0:S], early_codes[:, S : 2 * S], late_codes[:]]
+        halves = [slice(0, H), slice(H, S)]
+        for h, half in enumerate(halves):
+            nc.vector.tensor_copy(
+                w_spread[:, half].rearrange("p (c h r) -> p c h r", h=2, r=16),
+                w_turned[:].rearrange("p (h c) -> p c h", h=2)[:, 8 * h : 8 * (h + 1), :].unsqueeze(3).to_broadcast([P, 8, 2, 16]),
+            )
+        for half in halves:
+            nc.vector.transpose(weight[:, half], w_spread[:, half])
 
-        mix(False, c_mix[1][:, 0:C_SPLIT, :], c_raw[1][:, :, 0:C_SPLIT])
-        mix(True, c_mix[1][:, C_SPLIT:S, :], c_raw[1][:, :, C_SPLIT:S])
-        quantise(c_codes[1][:], c_scale[1][:], c_mix[1][:])
+        def gather(n, lo, hi):
+            listed = offsets[:, lo // 16 : hi // 16]
+            nc.vector.tensor_tensor(picked[n // 4][:, n % 4, lo:hi], planes[n][:].indirect(listed), weight[:, lo:hi], MULT)
 
-        for a in range(NX):
+        x_codes, c_codes = {}, {}
+        last = NX - 1
+        for half in halves:
+            gather(0, half.start, half.stop)
+        for n in range(1, PLANES - 1):
+            gather(n, 0, S)
+            if n in (3, 7):
+                mix(True, x_mix[n // 4], picked[n // 4][:])
+            if n in C_BEHIND:
+                mix(True, c_mix[C_BEHIND.index(n)], c_raw[C_BEHIND.index(n)][:])
+            if n == C_BEHIND[0]:
+                x_codes[0] = held([P, S], U32, "x_codes0", "plane%d" % n)[:]
+                quantise(x_codes[0], x_scale[0], x_mix[0])
+            if n == C_BEHIND[1]:
+                both_codes = held([P, 2 * S], U32, "both_codes", "plane%d" % n)
+                quantise(both_codes[:], both_scale[:], both_mix[:])
+                x_codes[1], c_codes[0] = both_codes[:, 0:S], both_codes[:, S : 2 * S]
+        for half in halves:
+            gather(PLANES - 1, half.start, half.stop)
+        late_codes = held([P, 2 * S], U32, "late_codes", "plane%d" % (PLANES - 1))
+        c_codes[1], x_codes[last] = late_codes[:, 0:S], late_codes[:, S : 2 * S]
+        quantise(c_codes[1], c_scale[1], c_mix[1])
+        for h, half in enumerate(halves):
+            mix(h == 0, late_mix[h][:], picked[last][:, :, half])
+        for h, half in enumerate(halves):
+            quantise(x_codes[last][:, half], x_scale[last][:, half], late_mix[h][:])
+
+        def times_w4(a, part, lo, hi):
+            m = part[0]
+            tile = w_first[:, a, :] if a == 0 else w_rest[:, a - 1, :]
+            fixed = tile[:, 2 * P * m : 2 * P * (m + 1)].bitcast(FP4X4)
+            multiply(part, lo, hi, fixed, w_scale[:, a, P * m : P * (m + 1)], x_codes[a], x_scale[a], start=a == 0)
+
+        for a in range(last):
             for part in parts:
-                m = part[0]
-                fixed = w_words[:, a, 2 * P * m : 2 * P * (m + 1)].bitcast(FP4X4)
-                multiply(part, fixed, w_scale[:, a, P * m : P * (m + 1)], x_codes[a], x_scale[:, S * a : S * (a + 1)], start=a == 0)
+                times_w4(a, part, part[1], part[2])
+        for half in halves:
+            for part in parts:
+                if part[1] <= half.start < part[2]:
+                    times_w4(last, part, half.start, half.stop)
 
         def u_pass(a, m):
             cols = slice(P * m, P * (m + 1))
@@ -162,16 +189,14 @@ def tile_list_hmix_gelu_kernel(tc, xT, w4_words, w4_scales, c, u, wgt, b, offs, 
             for part in parts:
                 left, right = part[1:]
                 if part[0] == m:
-                    multiply(part, u_codes[a][:, cols].bitcast(FP8X4), u_scale[a][:, cols], c_codes[a][:], c_scale[a][:], stop=a == NC - 1)
+                    multiply(part, left, right, u_codes[a][:, cols].bitcast(FP8X4), u_scale[a][:, cols], c_codes[a], c_scale[a], stop=a == NC - 1)
                     if a == NC - 1:
                         nc.scalar.activation(result[m][:, left:right], sums[part][:], GELU, bias=b_cols[:, 8 * m : 8 * m + 1])
                         nc.sync.dma_start(out[P * m : P * (m + 1), left:right], result[m][:, left:right])
 
         for m in range(NM):
-            mix(m > 0, u_mix[0][m][:], u_first[:, :, P * m : P * (m + 1)])
-        u_pass(0, 0)
+            mix(True, u_mix[0][m][:], u_first[:, :, P * m : P * (m + 1)])
         for m in range(NM):
             mix(False, u_mix[1][m][:], u_last[m][:])
-            if m + 1 < NM:
-                u_pass(0, m + 1)
+            u_pass(0, m)
             u_pass(1, m)

@@ -25,7 +25,8 @@ PLANES = 4 * NX
 
 SCALES_BEHIND = 7
 C_BEHIND = (6, 10)
-W_BEHIND = 10
+W_BEHIND = 11
+U_PIECES = ((0, 2), (2, 3), (3, 4))
 PAIRED = 2
 ON_SCALAR_QUEUE = (0,)
 
@@ -51,19 +52,20 @@ def tile_list_hmix_gelu_kernel(tc, xT, w4_words, w4_scales, c, u, wgt, b, offs, 
         picked = [held([P, 4, S], F32, "picked%d" % a) for a in range(NX)]
         c_raw = [held([P, 4, S], F32, "c_raw%d" % a) for a in range(NC)]
         u_first = held([P, 4, M], F32, "u_first")
-        u_last = [held([P, 4, P], F32, "u_last%d" % m) for m in range(NM)]
+        u_last = [held([P, 4, P * (hi - lo)], F32, "u_last%d" % lo) for lo, hi in U_PIECES]
         both_mix = held([P, 2 * S, 4], BF16, "both_mix")
         both_scale = held([P, 2 * S], U8, "both_scale")
         x_mix = [held([P, S, 4], BF16, "x_mix0")[:], both_mix[:, 0:S, :]]
         late_mix = [held([P, H, 4], BF16, "late_mix%d" % h) for h in range(2)]
         c_mix = [both_mix[:, S : 2 * S, :], held([P, S, 4], BF16, "c_mix1")[:]]
-        u_mix = [[held([P, P, 4], BF16, "u_mix%d_%d" % (a, m)) for m in range(NM)] for a in range(NC)]
+        first_mix = [held([P, 2 * P, 4], BF16, "first_mix0"), held([P, P, 4], BF16, "first_mix2"), held([P, P, 4], BF16, "first_mix3")]
         x_scale = [held([P, S], U8, "x_scale0")[:], both_scale[:, 0:S], held([P, S], U8, "x_scale2")[:]]
         c_scale = [both_scale[:, S : 2 * S], held([P, S], U8, "c_scale1")[:]]
         u_codes = [held([P, M], U32, "u_codes%d" % a) for a in range(NC)]
         u_scale = [held([P, M], U8, "u_scale%d" % a) for a in range(NC)]
         w_first = held([P, 1, 2 * M], U8, "w_first")
-        w_rest = held([P, NX - 1, 2 * M], U8, "w_rest")
+        w_rest = held([P, NX - 1, 2 * P * (NM - 1)], U8, "w_rest")
+        w_tail = held([P, NX - 1, 2 * P], U8, "w_tail")
         w_scale = held([P, NX, M], U8, "w_scale")
         result = [held([P, S], F32, "result%d" % m) for m in range(NM)]
         parts = [(0, 0, S), (1, 0, S), (2, 0, S), (3, 0, H), (3, H, S)]
@@ -120,23 +122,21 @@ def tile_list_hmix_gelu_kernel(tc, xT, w4_words, w4_scales, c, u, wgt, b, offs, 
                         w_scale[r:P:32, :, :].bitcast(I32),
                         w4_scales[:, r:16:4, :].rearrange("a q n -> q a n").bitcast(I32),
                     )
-        nc.sync.dma_start(w_rest[:], words[:, 1:NX, :])
+        nc.sync.dma_start(w_rest[:], words[:, 1:NX, 0 : 2 * P * (NM - 1)])
         load_rows(u_first, u, 0, 0, M)
-        for m in range(NM):
-            load_rows(u_last[m], u, 1, P * m, P * (m + 1))
+        for piece, (lo, hi) in enumerate(U_PIECES):
+            load_rows(u_last[piece], u, 1, P * lo, P * hi)
+        nc.sync.dma_start(w_tail[:], words[:, 1:NX, 2 * P * (NM - 1) : 2 * M])
 
         nc.scalar.activation(warm[:], warm[:], GELU)
         nc.scalar.copy(planes[PAIRED + 1][:], planes[PAIRED][:, T : 2 * T])
         nc.vector.transpose(w_turned[:], w_dealt[:])
         nc.vector.transpose(b_cols[:], b_dealt[:])
-        halves = [slice(0, H), slice(H, S)]
-        for h, half in enumerate(halves):
-            nc.vector.tensor_copy(
-                w_spread[:, half].rearrange("p (c h r) -> p c h r", h=2, r=16),
-                w_turned[:].rearrange("p (h c) -> p c h", h=2)[:, 8 * h : 8 * (h + 1), :].unsqueeze(3).to_broadcast([P, 8, 2, 16]),
-            )
-        for half in halves:
-            nc.vector.transpose(weight[:, half], w_spread[:, half])
+        nc.vector.tensor_copy(
+            w_spread[:].rearrange("p (c h r) -> p c h r", h=2, r=16),
+            w_turned[:].rearrange("p (h c) -> p c h", h=2).unsqueeze(3).to_broadcast([P, 16, 2, 16]),
+        )
+        nc.vector.transpose(weight[:], w_spread[:])
 
         def gather(n, lo, hi):
             listed = offsets[:, lo // 16 : hi // 16]
@@ -144,9 +144,7 @@ def tile_list_hmix_gelu_kernel(tc, xT, w4_words, w4_scales, c, u, wgt, b, offs, 
 
         x_codes, c_codes = {}, {}
         last = NX - 1
-        for half in halves:
-            gather(0, half.start, half.stop)
-        for n in range(1, PLANES - 1):
+        for n in range(PLANES - 1):
             gather(n, 0, S)
             if n in (3, 7):
                 mix(True, x_mix[n // 4], picked[n // 4][:])
@@ -159,6 +157,7 @@ def tile_list_hmix_gelu_kernel(tc, xT, w4_words, w4_scales, c, u, wgt, b, offs, 
                 both_codes = held([P, 2 * S], U32, "both_codes", "plane%d" % n)
                 quantise(both_codes[:], both_scale[:], both_mix[:])
                 x_codes[1], c_codes[0] = both_codes[:, 0:S], both_codes[:, S : 2 * S]
+        halves = [slice(0, H), slice(H, S)]
         for half in halves:
             gather(PLANES - 1, half.start, half.stop)
         late_codes = held([P, 2 * S], U32, "late_codes", "plane%d" % (PLANES - 1))
@@ -171,32 +170,59 @@ def tile_list_hmix_gelu_kernel(tc, xT, w4_words, w4_scales, c, u, wgt, b, offs, 
 
         def times_w4(a, part, lo, hi):
             m = part[0]
-            tile = w_first[:, a, :] if a == 0 else w_rest[:, a - 1, :]
-            fixed = tile[:, 2 * P * m : 2 * P * (m + 1)].bitcast(FP4X4)
-            multiply(part, lo, hi, fixed, w_scale[:, a, P * m : P * (m + 1)], x_codes[a], x_scale[a], start=a == 0)
+            if a > 0 and m == NM - 1:
+                fixed = w_tail[:, a - 1, :]
+            else:
+                fixed = (w_rest[:, a - 1, :] if a > 0 else w_first[:, 0, :])[:, 2 * P * m : 2 * P * (m + 1)]
+            multiply(part, lo, hi, fixed.bitcast(FP4X4), w_scale[:, a, P * m : P * (m + 1)], x_codes[a], x_scale[a], start=a == 0)
 
         for a in range(last):
             for part in parts:
-                times_w4(a, part, part[1], part[2])
+                if a == 0 or part[0] < NM - 1:
+                    times_w4(a, part, part[1], part[2])
         for half in halves:
-            for part in parts:
-                if part[1] <= half.start < part[2]:
-                    times_w4(last, part, half.start, half.stop)
+            for part in parts[: NM - 1]:
+                times_w4(last, part, half.start, half.stop)
 
-        def u_pass(a, m):
-            cols = slice(P * m, P * (m + 1))
-            quantise(u_codes[a][:, cols], u_scale[a][:, cols], u_mix[a][m][:])
+        def u_pass(a, lo, hi, values):
+            quantise(u_codes[a][:, P * lo : P * hi], u_scale[a][:, P * lo : P * hi], values)
             for part in parts:
-                left, right = part[1:]
-                if part[0] == m:
+                m, left, right = part
+                if lo <= m < hi:
+                    cols = slice(P * m, P * (m + 1))
                     multiply(part, left, right, u_codes[a][:, cols].bitcast(FP8X4), u_scale[a][:, cols], c_codes[a], c_scale[a], stop=a == NC - 1)
                     if a == NC - 1:
                         nc.scalar.activation(result[m][:, left:right], sums[part][:], GELU, bias=b_cols[:, 8 * m : 8 * m + 1])
                         nc.sync.dma_start(out[P * m : P * (m + 1), left:right], result[m][:, left:right])
 
-        for m in range(NM):
-            mix(True, u_mix[0][m][:], u_first[:, :, P * m : P * (m + 1)])
-        for m in range(NM):
-            mix(False, u_mix[1][m][:], u_last[m][:])
-            u_pass(0, m)
-            u_pass(1, m)
+        def first_values(lo, hi):
+            piece = max(lo - 1, 0)
+            base = U_PIECES[piece][0]
+            return first_mix[piece][:, P * (lo - base) : P * (hi - base), :]
+
+        def mix_first(m, on_scalar):
+            mix(on_scalar, first_values(m, m + 1), u_first[:, :, P * m : P * (m + 1)])
+
+        def mix_last(m, on_scalar, tag=None):
+            values = held([P, P, 4], BF16, "last_mix%d" % m, tag)
+            piece = max(m - 1, 0)
+            lo = P * (m - U_PIECES[piece][0])
+            mix(on_scalar, values[:], u_last[piece][:, :, lo : lo + P])
+            return values[:]
+
+        for m in range(3):
+            mix_first(m, m > 0)
+        second = mix_last(1, True)
+        mix_first(3, True)
+        u_pass(0, 0, 2, first_values(0, 2))
+        values = mix_last(0, False)
+        u_pass(0, 2, 3, first_values(2, 3))
+        u_pass(1, 0, 1, values)
+        u_pass(1, 1, 2, second)
+        values = mix_last(2, False, "u_last0")
+        u_pass(0, 3, 4, first_values(3, 4))
+        u_pass(1, 2, 3, values)
+        for part in parts[NM - 1 :]:
+            for a in range(1, NX):
+                times_w4(a, part, part[1], part[2])
+        u_pass(1, 3, 4, mix_last(3, False, "u_first"))

from contextlib import ExitStack

import concourse.mybir as mybir

K, L, M, T, S = 1536, 1024, 512, 1024, 512
FLOPS = 2 * M * S * (K + L)

F32 = mybir.dt.float32
BF16 = mybir.dt.bfloat16
I32 = mybir.dt.int32
U32 = mybir.dt.uint32
U16 = mybir.dt.uint16
U8 = mybir.dt.uint8
FP8X4 = mybir.dt.float8_e4m3fn_x4
FP4X4 = mybir.dt.float4_e2m1fn_x4
MULT = mybir.AluOpType.mult
GELU = mybir.ActivationFunctionType.Gelu_apprx_tanh

P = 128
KP = 512
NX, NC = K // KP, L // KP
NM = M // P
H = S // 2
PLANES = 4 * NX

SCALES_BEHIND = 7
C_BEHIND = (6, 10)
W_BEHIND = 11
U_PIECES = ((0, 2), (2, 3), (3, 4))
PAIRED = 2
ON_SCALAR_QUEUE = (0,)


def tile_list_hmix_gelu_kernel(tc, xT, w4_words, w4_scales, c, u, wgt, b, offs, out):
    nc = tc.nc
    with ExitStack() as ctx:
        keep = ctx.enter_context(tc.tile_pool(name="keep", bufs=1))
        psum = ctx.enter_context(tc.psum_pool(name="psum", bufs=1))

        def held(shape, dtype, name, tag=None):
            return keep.tile(shape, dtype, name=name, tag=tag or name, align_bytes=64)

        offsets = keep.tile([P, S // 16], U16, name="offsets")
        w_dealt = held([P, 32], F32, "w_dealt")
        w_turned = held([P, 32], F32, "w_turned")
        w_spread = held([P, S], F32, "w_spread")
        weight = held([P, S], F32, "weight")
        b_dealt = held([P, 32], F32, "b_dealt")
        b_cols = held([P, 32], F32, "b_cols")
        warm = held([P, 1], F32, "warm")
        planes = [held([P, 2 * T if n == PAIRED else T], F32, "plane%d" % n) for n in range(PLANES)]
        picked = [held([P, 4, S], F32, "picked%d" % a) for a in range(NX)]
        c_raw = [held([P, 4, S], F32, "c_raw%d" % a) for a in range(NC)]
        u_first = held([P, 4, M], F32, "u_first")
        u_last = [held([P, 4, P * (hi - lo)], F32, "u_last%d" % lo) for lo, hi in U_PIECES]
        both_mix = held([P, 2 * S, 4], BF16, "both_mix")
        both_scale = held([P, 2 * S], U8, "both_scale")
        x_mix = [held([P, S, 4], BF16, "x_mix0")[:], both_mix[:, 0:S, :]]
        late_mix = [held([P, H, 4], BF16, "late_mix%d" % h) for h in range(2)]
        c_mix = [both_mix[:, S : 2 * S, :], held([P, S, 4], BF16, "c_mix1")[:]]
        first_mix = [held([P, 2 * P, 4], BF16, "first_mix0"), held([P, P, 4], BF16, "first_mix2"), held([P, P, 4], BF16, "first_mix3")]
        x_scale = [held([P, S], U8, "x_scale0")[:], both_scale[:, 0:S], held([P, S], U8, "x_scale2")[:]]
        c_scale = [both_scale[:, S : 2 * S], held([P, S], U8, "c_scale1")[:]]
        u_codes = [held([P, M], U32, "u_codes%d" % a) for a in range(NC)]
        u_scale = [held([P, M], U8, "u_scale%d" % a) for a in range(NC)]
        w_first = held([P, 1, 2 * M], U8, "w_first")
        w_rest = held([P, NX - 1, 2 * P * (NM - 1)], U8, "w_rest")
        w_tail = held([P, NX - 1, 2 * P], U8, "w_tail")
        w_scale = held([P, NX, M], U8, "w_scale")
        result = [held([P, S], F32, "result%d" % m) for m in range(NM)]
        parts = [(0, 0, S), (1, 0, S), (2, 0, S), (3, 0, H), (3, H, S)]
        sums = {part: psum.tile([P, part[2] - part[1]], F32, name="sums%d_%d" % part[:2]) for part in parts}

        def load_rows(tile, src, a, lo, hi):
            rows = src[KP * a : KP * (a + 1), :].rearrange("(p i) w -> p i w", i=4)
            nc.sync.dma_start(tile[:], rows[:, :, lo:hi])

        def mix(on_scalar, dst, src):
            src = src.rearrange("p i (g w) -> p g i w", w=4)
            dst = dst.rearrange("p (g w) i -> p g i w", w=4)
            if on_scalar:
                nc.scalar.copy(dst, src)
            else:
                nc.vector.tensor_copy(dst, src)

        def quantise(words, scale, values):
            nc.vector.quantize_mx(out=words.bitcast(FP8X4), scales=scale, in_=values.rearrange("p w i -> p (w i)"))

        def multiply(part, lo, hi, fixed, fixed_scale, moving, moving_scale, start=False, stop=False):
            nc.tensor.matmul_mx(
                out=sums[part][:, lo - part[1] : hi - part[1]],
                lhsT=fixed,
                lhsT_scale=fixed_scale,
                rhs=moving[:, lo:hi].bitcast(FP8X4),
                rhs_scale=moving_scale[:, lo:hi],
                start=start,
                stop=stop,
            )

        nc.gpsimd.memset(b_dealt[:], 0.0)
        nc.gpsimd.memset(warm[:], 0.0)
        nc.gpsimd.memset(w_scale[:].rearrange("p a n -> p (a n)").bitcast(I32), 0)

        nc.sync.dma_start(w_dealt[:], wgt.rearrange("r (h w) -> (r h) w", h=2)[0 : 2 * P : 17, :])
        nc.sync.dma_start(b_dealt[0:P:8, :], b.rearrange("(m q w) -> q m w", q=4, w=32))
        nc.sync.dma_start(offsets[:], offs)
        words = w4_words.rearrange("a p n -> p a n")
        for n in range(PLANES):
            rows = xT[KP * (n // 4) : KP * (n // 4 + 1), :].rearrange("(p i) t -> p i t", i=4)
            queue = nc.scalar if n in ON_SCALAR_QUEUE else nc.sync
            if n == PAIRED:
                queue.dma_start(planes[n][:], rows[:, n % 4 : n % 4 + 2, :].rearrange("p i t -> p (i t)"))
            elif n != PAIRED + 1:
                queue.dma_start(planes[n][:], rows[:, n % 4, :])
            if n in C_BEHIND:
                load_rows(c_raw[C_BEHIND.index(n)], c, C_BEHIND.index(n), 0, S)
            if n == W_BEHIND:
                nc.sync.dma_start(w_first[:], words[:, 0:1, :])
            if n == SCALES_BEHIND:
                for r in range(4):
                    nc.sync.dma_start(
                        w_scale[r:P:32, :, :].bitcast(I32),
                        w4_scales[:, r:16:4, :].rearrange("a q n -> q a n").bitcast(I32),
                    )
        nc.sync.dma_start(w_rest[:], words[:, 1:NX, 0 : 2 * P * (NM - 1)])
        load_rows(u_first, u, 0, 0, M)
        for piece, (lo, hi) in enumerate(U_PIECES):
            load_rows(u_last[piece], u, 1, P * lo, P * hi)
        nc.sync.dma_start(w_tail[:], words[:, 1:NX, 2 * P * (NM - 1) : 2 * M])

        nc.scalar.activation(warm[:], warm[:], GELU)
        nc.scalar.copy(planes[PAIRED + 1][:], planes[PAIRED][:, T : 2 * T])
        nc.vector.transpose(w_turned[:], w_dealt[:])
        nc.vector.transpose(b_cols[:], b_dealt[:])
        nc.vector.tensor_copy(
            w_spread[:].rearrange("p (c h r) -> p c h r", h=2, r=16),
            w_turned[:].rearrange("p (h c) -> p c h", h=2).unsqueeze(3).to_broadcast([P, 16, 2, 16]),
        )
        nc.vector.transpose(weight[:], w_spread[:])

        def gather(n, lo, hi):
            listed = offsets[:, lo // 16 : hi // 16]
            nc.vector.tensor_tensor(picked[n // 4][:, n % 4, lo:hi], planes[n][:].indirect(listed), weight[:, lo:hi], MULT)

        x_codes, c_codes = {}, {}
        last = NX - 1
        for n in range(PLANES - 1):
            gather(n, 0, S)
            if n in (3, 7):
                mix(True, x_mix[n // 4], picked[n // 4][:])
            if n in C_BEHIND:
                mix(True, c_mix[C_BEHIND.index(n)], c_raw[C_BEHIND.index(n)][:])
            if n == C_BEHIND[0]:
                x_codes[0] = held([P, S], U32, "x_codes0", "plane%d" % n)[:]
                quantise(x_codes[0], x_scale[0], x_mix[0])
            if n == C_BEHIND[1]:
                both_codes = held([P, 2 * S], U32, "both_codes", "plane%d" % n)
                quantise(both_codes[:], both_scale[:], both_mix[:])
                x_codes[1], c_codes[0] = both_codes[:, 0:S], both_codes[:, S : 2 * S]
        halves = [slice(0, H), slice(H, S)]
        for half in halves:
            gather(PLANES - 1, half.start, half.stop)
        late_codes = held([P, 2 * S], U32, "late_codes", "plane%d" % (PLANES - 1))
        c_codes[1], x_codes[last] = late_codes[:, 0:S], late_codes[:, S : 2 * S]
        quantise(c_codes[1], c_scale[1], c_mix[1])
        for h, half in enumerate(halves):
            mix(h == 0, late_mix[h][:], picked[last][:, :, half])
        for h, half in enumerate(halves):
            quantise(x_codes[last][:, half], x_scale[last][:, half], late_mix[h][:])

        def times_w4(a, part, lo, hi):
            m = part[0]
            if a > 0 and m == NM - 1:
                fixed = w_tail[:, a - 1, :]
            else:
                fixed = (w_rest[:, a - 1, :] if a > 0 else w_first[:, 0, :])[:, 2 * P * m : 2 * P * (m + 1)]
            multiply(part, lo, hi, fixed.bitcast(FP4X4), w_scale[:, a, P * m : P * (m + 1)], x_codes[a], x_scale[a], start=a == 0)

        for a in range(last):
            for part in parts:
                if a == 0 or part[0] < NM - 1:
                    times_w4(a, part, part[1], part[2])
        for half in halves:
            for part in parts[: NM - 1]:
                times_w4(last, part, half.start, half.stop)

        def u_pass(a, lo, hi, values):
            quantise(u_codes[a][:, P * lo : P * hi], u_scale[a][:, P * lo : P * hi], values)
            for part in parts:
                m, left, right = part
                if lo <= m < hi:
                    cols = slice(P * m, P * (m + 1))
                    multiply(part, left, right, u_codes[a][:, cols].bitcast(FP8X4), u_scale[a][:, cols], c_codes[a], c_scale[a], stop=a == NC - 1)
                    if a == NC - 1:
                        nc.scalar.activation(result[m][:, left:right], sums[part][:], GELU, bias=b_cols[:, 8 * m : 8 * m + 1])
                        nc.sync.dma_start(out[P * m : P * (m + 1), left:right], result[m][:, left:right])

        def first_values(lo, hi):
            piece = max(lo - 1, 0)
            base = U_PIECES[piece][0]
            return first_mix[piece][:, P * (lo - base) : P * (hi - base), :]

        def mix_first(m, on_scalar):
            mix(on_scalar, first_values(m, m + 1), u_first[:, :, P * m : P * (m + 1)])

        def mix_last(m, on_scalar, tag=None):
            values = held([P, P, 4], BF16, "last_mix%d" % m, tag)
            piece = max(m - 1, 0)
            lo = P * (m - U_PIECES[piece][0])
            mix(on_scalar, values[:], u_last[piece][:, :, lo : lo + P])
            return values[:]

        for m in range(3):
            mix_first(m, m > 0)
        second = mix_last(1, True)
        mix_first(3, True)
        u_pass(0, 0, 2, first_values(0, 2))
        values = mix_last(0, False)
        u_pass(0, 2, 3, first_values(2, 3))
        u_pass(1, 0, 1, values)
        u_pass(1, 1, 2, second)
        values = mix_last(2, False, "u_last0")
        u_pass(0, 3, 4, first_values(3, 4))
        u_pass(1, 2, 3, values)
        for part in parts[NM - 1 :]:
            for a in range(1, NX):
                times_w4(a, part, part[1], part[2])
        u_pass(1, 3, 4, mix_last(3, False, "u_first"))
